import numpy as np, ml_dtypes
CORES = [23,119,17,113]
N = 4
BF = ml_dtypes.bfloat16
P, S, M, RO = 1024, 4, 4, 6
W, E, Q = N * P, P // S, 2 ** M
def pack(nm, mk):
    z = (nm << M) | mk
    return {"kin": np.ascontiguousarray(z.reshape(128, N, P).transpose(1, 0, 2)).astype(np.int32)}
def town(rng, caps, nin, skew=False):
    order = rng.permutation(W); pos = np.empty(W, np.int64); pos[order] = np.arange(W); blk = pos >> 6; nb = W >> 6
    if skew: key = rng.standard_exponential((8, W, 64), dtype=np.float32) * np.exp2(np.arange(64) * 0.125).astype(np.float32)
    else: key = rng.random((8, W, 64), dtype=np.float32) + 2 * (np.arange(64) >= rng.choice(np.array(caps), nb)[blk][:, None]).astype(np.float32)
    inn = order[64 * blk[None, :, None] + np.argsort(key, axis=-1)[..., :16]]
    ob = (blk + 1 + rng.integers(0, nb - 1, (8, W))) % nb
    far = (rng.integers(0, 64, (8, W, 1)) + (2 * rng.integers(0, 32, (8, W, 1)) + 1) * np.arange(16)) & 63
    m = np.argsort(rng.random((8, W, 16)), axis=-1) < rng.choice(np.array(nin), nb)[blk][None, :, None]
    return np.ascontiguousarray(np.where(m, inn, order[64 * ob[..., None] + far]).transpose(0, 2, 1))
def flips(rng, q):
    f = np.zeros((8, 16, W), np.int64)
    for m in range(M): f |= (rng.random((8, 16, W), dtype=np.float32) < q).astype(np.int64) << m
    return f
def marks(rng, nm, shares):
    lab = rng.integers(0, Q, W)
    return lab[None, None, :] ^ lab[nm] ^ flips(rng, rng.choice(np.array(shares), (8, 1, W)))
def setup_inputs(rng):
    nm = town(rng, [20, 32, 48, 64], [8, 10, 12, 14, 15])
    return pack(nm, marks(rng, nm, [0.05, 0.2, 0.5]))
def setup_inputs_spread(rng):
    nm = town(rng, [64], [9, 12, 14], True); k = np.argsort(rng.random((8, 16, W)), axis=1)
    wide_ = (rng.integers(0, W, (8, 1, W)) + k * rng.integers(1, W // 16, (8, 1, W))) % W
    nm = np.where(rng.random((8, 1, W)) < 0.33, wide_, nm)
    return pack(nm, flips(rng, rng.choice(np.array([0.02, 0.1, 0.5, 0.9, 0.98]), (8, 1, W))))
def setup_inputs_ends(rng):
    e = np.concatenate([np.arange(8), np.arange(W - 8, W)]); x = np.array([8, 9, W - 10, W - 9]); pool = np.concatenate([e, x])
    full = rng.random(W) < 0.5; kind = rng.integers(0, 6, W)
    for r in range(N): kind[P * r + P - 22:P * r + P] = (np.arange(22) + r) % 6
    full[e] = True; full[x] = False; kind[e] = 0; kind[x] = 4
    idx = np.where(full[None, :, None], np.argsort(rng.random((8, W, 16)), axis=-1), np.argsort(rng.random((8, W, 20)), axis=-1)[..., :16])
    nm = np.ascontiguousarray(pool[idx].transpose(0, 2, 1))
    lab = rng.integers(0, 2, W); lab[0] = 0; lab[W - 1] = 1
    half = np.broadcast_to((np.argsort(rng.random((8, W)), axis=0) < 4)[:, None, :], (8, 16, W))
    spot = np.arange(128).reshape(8, 16, 1) == np.where(rng.random(W) < 0.5, 127, rng.integers(0, 128, W))[None, None, :]
    f = np.zeros((8, 16, W), bool)
    for c, v in ((1, half), (2, half & ~spot), (3, half | spot), (4, rng.random((8, 16, W)) < 0.5), (5, ~spot)): f = np.where(kind == c, v, f)
    return pack(nm, (lab[None, None, :] ^ lab[nm] ^ f.astype(np.int64)) * (Q - 1))
def setup_inputs_crowd(rng):
    rot = rng.permutation(N)
    order = np.ascontiguousarray((np.argsort(rng.random((N, P)), axis=1) + P * rot[:, None]).reshape(N, P >> 4, 16).transpose(1, 0, 2)).reshape(-1)
    pos = np.empty(W, np.int64); pos[order] = np.arange(W); blk = pos // (16 * N); lay = (pos >> 4) % N; nb = P >> 4
    typ = (rng.permutation(nb) % 3)[blk]
    p = (16 * N * blk + 16 * np.where(typ == 2, 0, (lay + 1) % N))[None, :, None] + np.argsort(rng.random((8, W, 16)), axis=-1)
    gs = rng.integers(0, 8, (nb, N))[blk, lay]; js = rng.integers(0, 16, (nb, N))[blk, lay]
    hit = (typ == 1)[None, :] & (np.arange(8)[:, None] == gs[None, :]) & ((pos & 15) == js)[None, :]
    nm = np.ascontiguousarray(order[np.where(hit[..., None], (p + 16 * N) % W, p)].transpose(0, 2, 1))
    pat = np.argsort(rng.random((nb, 8, M)), axis=1) < rng.choice(np.array([0, 3, 4, 5, 8]), (nb, 1, M))
    u = np.sum(pat.astype(np.int64) << np.arange(M), axis=2)[blk].T
    on = np.where(typ == 2, lay > 0, (lay & 1) == 0)
    noise = np.where(rng.random((8, 16, W)) < (rng.choice(np.array([0.0, 0.04]), nb)[blk])[None, None, :], rng.integers(0, Q, (8, 16, W)), 0)
    return pack(nm, np.where(on[None, :], u, 0)[:, None, :] ^ noise)
def put(a, k, v, on):
    w = a[k].copy(); a[:] = np.where((a == v) & on, w, a); a[k] = np.where(on, v, a[k])
def setup_inputs_corners(rng):
    nm = town(rng, [20, 40, 64], [10, 13]); p = np.arange(W); every = np.ones(W, bool)
    nm[7] = (p + 1 + np.argsort(rng.random((16, W)), axis=0)) % W
    nm[6] = (p + W - 8 + np.argsort(rng.random((16, W)), axis=0)) % W
    put(nm[0], 0, p, every)
    on = ((p >> 5) & 1) == rng.integers(0, 2)
    put(nm[1], 1, (p + 1) % W, on); put(nm[1], 4, (p + W - 1) % W, on)
    put(nm[2], 2, np.where(rng.random(W) < 0.5, 0, W - 1), every)
    put(nm[2], 5, np.where(p == 0, W - 1, 0), (p == 0) | (p == W - 1))
    put(nm[3], 3, (p + 1) % W, every); put(nm[3], 6, (p + 2) % W, every)
    put(nm[4], 15, np.zeros(W, np.int64), every); put(nm[5], 15, np.full(W, W - 1), every); put(nm[5], 0, np.zeros(W, np.int64), rng.random(W) < 0.5)
    kind = rng.integers(0, 4, (8, W >> 5))[:, p >> 5][:, None, :]
    mk = marks(rng, nm, [0.0, 0.1]); rnd = rng.integers(0, Q, (8, 16, W))
    return pack(nm, np.where(kind == 0, 0, np.where(kind == 1, Q - 1, np.where(kind == 2, mk, rnd))))
def setup_inputs_calm(rng):
    nm = town(rng, [64], [2, 3, 4, 5, 6]); p = np.arange(W); i = rng.permutation(E - 1)[:9]
    one = np.add.outer(P * np.arange(N), S * i[:8]).reshape(-1); two = one + 1
    h = P * int(rng.integers(0, N)) + S * int(i[8])
    on1 = np.zeros(W, bool); on1[one] = True
    on2 = np.zeros(W, bool); on2[two] = True
    for g in range(8):
        put(nm[g], 15, W - 1, on1)
        for j in range(8): put(nm[g], 4 + j, P * ((p // P + 1) % N) + S * int(i[j]), on2)
    put(nm[0], 0, h, on1); put(nm[S], S, h, on1); put(nm[1], 1, h, on2)
    put(nm[0], 0, h + 1, p == h); put(nm[0], 3, W - 1, p == h); put(nm[1], 4, W - 1, p == h); put(nm[S], S + 3, W - 1, p == h)
    put(nm[0], 3, h, p == h + 1)
    mk = marks(rng, nm, [0.1, 0.5])
    mk[:, 15, one] = np.where(np.argsort(rng.random((8, 8 * N)), axis=0) < 2, 0, Q - 1)
    mk[0, 0, one] = Q - 1; mk[S, S, one] = Q - 1; mk[:, 4:12, two] = 0
    mk[0, 3, h] = 0; mk[1, 4, h] = 0; mk[S, S + 3, h] = 0
    return pack(nm, mk)
def check_inputs(d):
    bad = []; z = np.asarray(d["kin"]).astype(np.int64)
    if np.min(z) < 0 or np.max(z) > Q * W - 1: bad.append("range of kin")
    s = np.sort((z >> M).reshape(N, 8, 16, P), axis=2)
    if np.any(s[:, :, 1:] == s[:, :, :-1]): bad.append("equal names in one list of kin")
    return bad
def reference(kin):
    z = np.ascontiguousarray(kin.astype(np.int64).transpose(1, 0, 2)).reshape(8, 16, W)
    for t in range(RO):
        a = np.add.outer(P * np.arange(N), S * np.arange(E) + t % S).reshape(-1)
        nm = z >> M; mk = z & (Q - 1)
        c = nm[t, t, a]; b = nm[t, t + 3, c]
        tes = np.zeros((8, 16, N * E), bool); own = np.zeros((8, 16, N * E), bool); val = np.zeros((8, 16, N * E), np.int64)
        for g in range(8):
            ca = nm[g][:, a]; ma = mk[g][:, a]
            eq = nm[g][:, ca] == b
            m2 = np.add.reduce(np.where(eq, mk[g][:, ca], 0), axis=0)
            own[g] = ca == b; tes[g] = np.any(eq, axis=0) | own[g]
            val[g] = np.where(own[g], ma, ma ^ m2)
        n = np.sum(tes.astype(np.int64), axis=(0, 1)); won = np.zeros(N * E, np.int64); dif = np.zeros((8, 16, N * E), np.int64)
        for m in range(M):
            bit = (val >> m) & 1
            w = (2 * np.sum(np.where(tes, bit, 0), axis=(0, 1)) > n).astype(np.int64)
            won = won + (w << m); dif = dif + (bit != w)
        key = np.where(own, 1000, np.where(tes, dif, -1))
        row = np.argmax(key, axis=1)
        gi, ai = np.nonzero(np.any(tes, axis=1) & (b != a))
        z[gi, row[gi, ai], a[ai]] = (Q * b + won)[ai]
    return {"yk": np.ascontiguousarray(z.reshape(128, N, P).transpose(1, 0, 2)).astype(np.float32)}

@@ -1,0 +1,611 @@
+import math
+from concourse.bass import DstId, RemoteDMATransfer
+from concourse.mybir import AluOpType, ActivationFunctionType
+
+A = AluOpType
+F = ActivationFunctionType
+RO = 6
+CFG = {
+    "parts": [(128, 0, 2), (128, 1, 2)],
+    "ks": [4, 4],
+    "kc": [0, 1],
+    "vw": 256,
+    "t4s": True, "prep": True, "evs": True, "split": True, "gap": 3000.0, "jit": 300.0, "tries": 24, "merge": False, "first": [1, 1],
+    "cyc": 1.0, "pe": 0.5, "gam": 1.56, "hop": 105.0, "xch": 4300.0,
+}
+BIG = 1.5 * 2.0 ** 27
+OFF = 24.5 / 16.0
+LN2 = math.log(2.0)
+
+
+def _sb(n, d):
+    return ("sbuf", [128, n], d)
+
+
+SCRATCH = {
+    "Z": _sb(1024, "int32"), "Tb": _sb(4096, "float32"), "Yo": _sb(1024, "float32"), "L": _sb(5 * 1024, "float32"),
+    "Dv": _sb(4096, "bfloat16"), "Cl": _sb(4096, "bfloat16"), "G": _sb(4096, "float32"),
+    "Of": _sb(256, "uint16"), "Gb": _sb(256, "float32"), "Bv": _sb(1024, "float32"), "Bh": _sb(256, "float16"),
+    "own": _sb(256, "bfloat16"), "skp": _sb(256, "bfloat16"), "pre": _sb(256, "float32"), "W": _sb(256, "int32"),
+    "Q": _sb(1024, "int32"), "E": _sb(1024, "bfloat16"), "tes": _sb(256, "bfloat16"), "won": _sb(256, "bfloat16"),
+    "Fd": _sb(1024, "bfloat16"), "U": _sb(256, "bfloat16"), "win": _sb(256, "float32"),
+    "zi": _sb(256, "int32"), "nm": _sb(256, "int32"), "i1": _sb(1024, "int32"), "ph": _sb(256, "float16"),
+    "pt": _sb(256, "float16"), "Aq": _sb(1024, "int32"), "at": _sb(256, "float32"), "Sel": _sb(256, "float32"),
+    "du": _sb(256, "float32"), "dn": _sb(256, "float32"),
+    "xc": _sb(144, "float32"), "xg": _sb(128, "float32"), "pw": _sb(128, "float32"), "ci": _sb(16, "int32"),
+    "cf": _sb(16, "float32"), "R64": _sb(144, "bfloat16"), "R16": _sb(144, "bfloat16"),
+    "If": _sb(128, "float32"), "Imf": _sb(128, "float32"), "I16f": _sb(128, "float32"), "Im15": _sb(128, "float32"),
+    "Ih": _sb(128, "float16"), "Im32": _sb(128, "bfloat16"), "I16": _sb(128, "bfloat16"), "I256": _sb(128, "bfloat16"),
+    "I8k": _sb(128, "bfloat16"), "Isk": _sb(128, "bfloat16"), "Ym": _sb(128, "bfloat16"),
+    "c1": _sb(128, "float32"), "c2": _sb(128, "float32"), "Pm": _sb(512, "float16"),
+    "Om": _sb(128, "bfloat16"), "Ob": _sb(128, "bfloat16"), "O16": _sb(128, "bfloat16"),
+    "Nw": _sb(256, "bfloat16"), "Vw": _sb(16, "bfloat16"), "Vm": _sb(16, "bfloat16"),
+}
+for _n in ("PD0", "PD1", "PW0", "PW1", "PA0", "PA1", "PX", "PM"):
+    SCRATCH[_n] = ("psum", [128, 512], "float32")
+NP = len(CFG["parts"])
+SEMAPHORES = (["ev", "es", "et", "eg", "lsI", "lsD", "arI"] + ["ld%d" % j for j in range(4)] + ["fw%d" % j for j in range(4)]
+              + ["st%d" % j for j in range(NP)]
+              + ["a%d_%d_%d" % (t, p, r) for t in range(RO - 1) for p in range(NP) for r in range(4)])
+ESEM = {"v": "ev", "s": "es", "t": "et", "g": "eg"}
+
+
+def _mask(engines):
+    m = 0
+    for e in engines:
+        m |= 1 << e
+    return m
+
+
+def _deps(ops):
+    lastw, readers, bank, deps = {}, {}, {}, []
+    for n, op in enumerate(ops):
+        d = set()
+        for k in op["r"]:
+            if k in lastw:
+                d.add(lastw[k])
+        for k in op["w"]:
+            if k in lastw:
+                d.add(lastw[k])
+            d.update(readers.get(k, []))
+        for k in set(k[:3] for k in op["r"] + op["w"] if k[0] == "P"):
+            b = bank.setdefault(k, [None, [], []])
+            if b[0] != op["e"]:
+                b[0], b[1], b[2] = op["e"], [], b[1]
+            d.update(b[2])
+            if op["e"] == "t" and b[1]:
+                d.add(b[1][-1])
+            b[1].append(n)
+        if op["k"] != "r":
+            for k in op["r"]:
+                readers.setdefault(k, []).append(n)
+        for k in op["w"]:
+            lastw[k] = n
+            readers[k] = []
+        d.discard(n)
+        deps.append(d)
+    return deps
+
+
+def _order(ops, deps, seed):
+    n = len(ops)
+    succ = [[] for _ in range(n)]
+    edges = [[(m, 0.0 if ops[m]["k"] == "w" or (ops[m]["e"] == "t" and ops[i]["e"] == "t") else ops[m]["lat"]) for m in deps[i]]
+             + list(ops[i]["after"]) for i in range(n)]
+    for i in range(n):
+        for m, l in edges[i]:
+            succ[m].append((i, l))
+    pr = [0.0] * n
+    for i in range(n - 1, -1, -1):
+        pr[i] = ops[i]["d"] + max([l + pr[j] for j, l in succ[i]] + [0.0])
+    x = seed
+    for i in range(n if seed else 0):
+        x = (x * 1103515245 + 12345) % 2147483648
+        pr[i] += CFG["jit"] * x / 2147483648.0
+    left = [len(e) for e in edges]
+    rdy = [0.0] * n
+    free = {}
+    ready = {}
+    for i in range(n):
+        if left[i] == 0:
+            ready.setdefault(ops[i]["e"], []).append(i)
+    order = []
+    while len(order) < n:
+        best = None
+        for e, l in ready.items():
+            if l:
+                t0 = max(free.get(e, 0.0), min(rdy[i] for i in l))
+                if best is None or t0 < best[0]:
+                    best = (t0, e)
+        t0, e = best
+        cand = [i for i in ready[e] if rdy[i] <= t0 + 1e-6]
+        i = max(cand, key=lambda j: (pr[j], -j))
+        soon = [j for j in ready[e] if t0 < rdy[j] < t0 + 0.5 * ops[i]["d"] and pr[j] > pr[i] + ops[i]["d"]]
+        if soon:
+            i = min(soon, key=lambda j: rdy[j])
+            t0 = rdy[i]
+        ready[e].remove(i)
+        order.append(i)
+        free[e] = t0 + ops[i]["d"]
+        for j, l in succ[i]:
+            rdy[j] = max(rdy[j], free[e] + l)
+            left[j] -= 1
+            if left[j] == 0:
+                ready.setdefault(ops[j]["e"], []).append(j)
+    return max(free.values()), order
+
+
+def _emit(g, T, ops):
+    qs = {"v": g.vector, "s": g.scalar, "t": g.tensor, "g": g, "y": g.sync}
+    deps = _deps(ops)
+    order = min(_order(ops, deps, x) for x in range(CFG["tries"]))[1]
+    pos = {i: p for p, i in enumerate(order)}
+    seen, waits = {}, {}
+    for i in order:
+        op, best = ops[i], {}
+        for m in deps[i]:
+            o = ops[m]
+            if o["k"] in "wr" or (o["e"] == "t" and op["e"] == "t"):
+                continue
+            key = o["e"] if o["k"] == "c" else m
+            if key not in best or pos[best[key]] < pos[m]:
+                best[key] = m
+        waits[i] = []
+        for key, m in best.items():
+            if seen.get((op["e"], key), -1) < pos[m]:
+                seen[(op["e"], key)] = pos[m]
+                waits[i].append(m)
+    need = set(m for w in waits.values() for m in w)
+    count, val = {}, {}
+    for i in order:
+        op = ops[i]
+        if op["k"] == "c" and i in need:
+            count[op["e"]] = count.get(op["e"], 0) + 1
+            val[i] = (ESEM[op["e"]], count[op["e"]])
+        elif op["k"] == "d":
+            val[i] = (op["sem"], 16)
+    for i in order:
+        op = ops[i]
+        q = qs[op["e"]]
+        for m in waits[i]:
+            q.wait_ge(T.sem[val[m][0]], val[m][1])
+        if op["k"] == "w":
+            for s, v in op["sems"]:
+                q.wait_ge(T.sem[s], v)
+            continue
+        ins = op["f"](q)
+        if i in val:
+            ins.then_inc(T.sem[val[i][0]], 16 if op["k"] == "d" else 1)
+
+
+def _helper(T, topo, core):
+    other = [c for c in T.cores if topo.chip(c) != topo.chip(core)][0]
+    return [c for c in topo.cores_of(other)
+            if T.rank_of(c) is None and topo.die(c) == topo.die(core) and topo.may_write(core, c)][0]
+
+
+def _hand_on(g, core, T, topo):
+    for src in T.cores:
+        if _helper(T, topo, src) != core:
+            continue
+        r = T.rank_of(src)
+        to = [c for c in T.cores if topo.chip(c) == topo.chip(core)]
+        es = topo.engines(core, to[0])
+        k = len(es) // len(to)
+        for j in range(4):
+            ap = T.Tb[:, 1024 * r + 256 * j:1024 * r + 256 * j + 256]
+            g.wait_ge(T.sem["fw%d" % j], len(topo.engines(src, core)))
+            g.remote_dma_fused([RemoteDMATransfer(dst_ids=[DstId(rid=topo.addr(c)[0], pnc=topo.addr(c)[1])],
+                                                  dma_engine_mask=_mask(es[k * x:k * x + k]), remote_sem=T.sem.arI, src=ap, dst=ap)
+                                for x, c in enumerate(to)], local_sem=T.sem.lsI)
+        g.wait_ge(T.sem.lsI, 4 * len(es))
+
+
+def rank_program(g, core, T, topo):
+    rank = T.rank_of(core)
+    if rank is None:
+        _hand_on(g, core, T, topo)
+        return
+    C = CFG
+    others = [c for c in T.cores if c != core]
+    sib = [c for c in others if topo.chip(c) == topo.chip(core)][0]
+    far = [c for c in others if topo.chip(c) != topo.chip(core)]
+    peer = [c for c in far if topo.die(c) == topo.die(core)][0]
+    e_far = topo.engines(core, peer)
+    e_all = topo.engines(core, sib)
+    e_near = [e for e in e_all if e not in e_far]
+    hf = len(e_far) // 2
+    plan3 = [(far[0], e_far[:hf]), (far[1], e_far[hf:]), (sib, e_near)]
+    prank, srank = T.rank_of(peer), T.rank_of(sib)
+    franks = [T.rank_of(c) for c in far]
+    ops = []
+
+    def op(e, f, r, w, d, k="c", lat=None, after=(), **kw):
+        o = {"e": e, "f": f, "r": list(r), "w": list(w), "k": k, "d": d, "lat": C["hop"] if lat is None else lat,
+             "after": list(after)}
+        o.update(kw)
+        ops.append(o)
+        return len(ops) - 1
+
+    def wait(e, sems, w, after=(), r=()):
+        return op(e, None, r, w, 0.0, k="w", sems=sems, after=after)
+
+    def dur(n, gth=False):
+        return 50.0 + n * C["gam"] * C["cyc"] if gth else max(64.0, n) * C["cyc"]
+
+    def ts(out, in0, s1, s2, o0, o1, r, w, n, gth=False):
+        if s2 is None:
+            op("v", lambda q: q.tensor_scalar(out, in0, s1, None, o0), r, w, dur(n, gth))
+        else:
+            op("v", lambda q: q.tensor_scalar(out, in0, s1, s2, o0, o1), r, w, dur(n, gth))
+
+    def tt(out, a, b, o, r, w, n, gth=False):
+        op("v", lambda q: q.tensor_tensor(out, a, b, o), r, w, dur(n, gth))
+
+    def act(out, in_, fn, bias, scale, r, w, n, gth=False):
+        op("s", lambda q: q.activation(out, in_, fn, bias=bias, scale=scale), r, w, dur(n, gth))
+
+    def mm(out, lhsT, rhs, start, stop, r, w, n, f32=False):
+        op("t", lambda q: q.matmul(out, lhsT, rhs, start, stop), r, w, max(64, n) * (4 if f32 else 1) * C["pe"], lat=C["hop"] + 45)
+
+    def iota(out, pat, base, cm, w, n, flt=True):
+        if flt:
+            op("g", lambda q: q.iota(out, pat, base, cm, allow_small_or_imprecise_dtypes=True), [], w, 130 + 2 * n * C["cyc"])
+        else:
+            op("g", lambda q: q.iota(out, pat, base, cm), [], w, 130 + 2 * n * C["cyc"])
+
+    def dst(c):
+        a = topo.addr(c)
+        return DstId(rid=a[0], pnc=a[1])
+
+    gq = [None]
+
+    def send(plan, ap, rsems, lsem, r, gap=0.0):
+        tr = [RemoteDMATransfer(dst_ids=[dst(c)], dma_engine_mask=_mask(es), remote_sem=T.sem[rs], src=ap, dst=ap)
+              for (c, es), rs in zip(plan, rsems)]
+        gq[0] = op("g", lambda q: q.remote_dma_fused(tr, local_sem=T.sem[lsem]), r, [], 500.0, k="r",
+                   after=[(gq[0], gap)] if gq[0] is not None else [])
+        return gq[0]
+
+    for j in range(4):
+        op("ys"[j % 2], lambda q, j=j: q.dma_start(T.Z[:, 256 * j:256 * j + 256], T.kin[:, 256 * j:256 * j + 256]),
+           [], ["Z%d" % j], 50.0, k="d", sem="ld%d" % j, lat=2500.0 + 400 * j)
+    iota(T.ci[:, 0:1], [[0, 1]], 0, 1, ["ci0"], 1, flt=False)
+    iota(T.xc[:], [[1, 144]], 0, 0, ["xc"], 144)
+    iota(T.pw[:], [[0, 128]], 0, 1, ["pw"], 128)
+    iota(T.xg[:], [[16, 8], [0, 16]], 0, 0, ["xg"], 128)
+    op("v", lambda q: q.memset(T.Vw[:], 0.0), [], ["Vw"], 64.0)
+    op("v", lambda q: q.memset(T.Vm[:], -1.0), [], ["Vm"], 64.0)
+    op("v", lambda q: q.memset(T.Vw[:, 3:4], 2.0), [], ["Vw"], 64.0)
+
+    def ci(j):
+        return T.ci[:, j:j + 1]
+
+    def cf(j):
+        return T.cf[:, j:j + 1]
+
+    for j, m in ((1, 112), (2, 16), (3, 15), (4, 1), (5, 2)):
+        ts(ci(j), ci(0), m, None, A.bitwise_and, None, ["ci0"], ["ci%d" % j], 1)
+    ts(cf(0), ci(0), 0.0, None, A.add, None, ["ci0"], ["cf0"], 1)
+    ts(cf(1), ci(1), 15.0, None, A.add, None, ["ci1"], ["cf1"], 1)
+    ts(cf(2), ci(1), 0.0, None, A.add, None, ["ci1"], ["cf2"], 1)
+    ts(cf(3), ci(2), 62.5, cf(0), A.mult, A.add, ["ci2", "cf0"], ["cf3"], 1)
+    ts(cf(4), ci(2), -62.5, cf(0), A.mult, A.add, ["ci2", "cf0"], ["cf4"], 1)
+    ts(cf(5), ci(3), -LN2, -LN2 * 336.0, A.mult, A.add, ["ci3"], ["cf5"], 1)
+    ts(cf(6), ci(5), 1.5, 1.0, A.mult, A.add, ["ci5"], ["cf6"], 1)
+    ts(cf(7), ci(4), 1.0, cf(6), A.add, A.mult, ["ci4", "cf6"], ["cf7"], 1)
+    ts(cf(8), cf(7), 0.0625, None, A.mult, None, ["cf7"], ["cf8"], 1)
+    x128 = T.xc[:, 0:128]
+    for c in range(2):
+        for gm in range(2):
+            sh = -16.0 * gm if c == 0 else -16.0 * (gm - 1) - 1000.0
+            j = 2 * c + gm
+            ts(T.Pm[:, 128 * j:128 * j + 128], x128, sh, cf(3 + c), A.add, A.is_equal, ["xc", "cf3", "cf4"], ["cPm%d" % j], 128)
+    eye = [("If", 1.0), ("Ih", -16.0), ("I8k", 8192.0), ("I16", 16.0), ("I256", 256.0), ("Isk", -1024.0),
+           ("I16f", 16.0), ("Im15", -15.0)]
+    if C["prep"]:
+        eye.append(("Imf", -1.0))
+    eye.append(("Im32", -32.0))
+    for nm, wgt in eye:
+        ts(T[nm][:], x128, cf(0), wgt, A.is_equal, A.mult, ["xc", "cf0"], [nm], 128)
+    ts(T.R64[:], T.xc[:], cf(1), 64.0, A.is_equal, A.mult, ["xc", "cf1"], ["R64"], 144)
+    if any(C["kc"]):
+        ts(T.R16[:], T.xc[:], cf(1), 16.0, A.is_equal, A.mult, ["xc", "cf1"], ["R16"], 144)
+    ts(T.c1[:], x128, cf(0), -2.0, A.is_equal, A.mult, ["xc", "cf0"], ["c1"], 128)
+    ts(T.c2[:], T.xg[:], cf(2), None, A.is_equal, None, ["xg", "cf2"], ["c2"], 128)
+    tt(T.Ym[:], T.c1[:], T.c2[:], A.add, ["c1", "c2"], ["Ym"], 256)
+    op("v", lambda q: q.memset(T.Om[:], -256.0), [], ["Om"], 64.0)
+    op("v", lambda q: q.memset(T.O16[:], 16.0), [], ["O16"], 64.0)
+    ts(T.c1[:], x128, cf(0), 49152.0, A.is_equal, A.mult, ["xc", "cf0"], ["c1"], 128)
+    ts(T.Ob[:], T.c1[:], 512.0, None, A.add, None, ["c1"], ["Ob"], 128)
+    ts(T.Nw[:, 0:128], T.pw[:], 0.0, cf(8), A.mult, A.add, ["pw", "cf8"], ["Nw0"], 128)
+    ts(T.Nw[:, 128:256], T.pw[:], 0.0, cf(7), A.mult, A.add, ["pw", "cf7"], ["Nw1"], 128)
+
+    PDk = [(T.PD0, "PD0"), (T.PD1, "PD1")]
+    OWN = ["To%d" % j for j in range(4)]
+    snd = []
+    for j in range(4):
+        pb, pk = PDk[j % 2]
+        zs, cs = T.Z[:, 256 * j:256 * j + 256], T.Tb[:, 1024 * rank + 256 * j:1024 * rank + 256 * j + 256]
+        i1 = T.i1[:, 256 * j:256 * j + 256]
+        ts(i1, zs, 15, None, A.bitwise_and, None, ["Z%d" % j], ["i1%d" % j], 256)
+        ts(pb[:, 0:256], i1, -0.9375, None, A.mult, None, ["i1%d" % j], [pk + "a"], 256)
+        tt(cs, zs, pb[:, 0:256], A.add, ["Z%d" % j, pk + "a"], [OWN[j]], 256)
+        snd.append(send([(_helper(T, topo, core), e_far), (sib, e_near)], cs, ["fw%d" % j, "arI"], "lsI", [OWN[j]]))
+    for e in "vs":
+        wait(e, [("arI", 4 * (len(e_near) + len(e_all))), ("lsI", 4 * len(e_all))], ["in" + e], after=[(gq[0], 9000.0)])
+
+    PA = [(T.PA0, "PA0"), (T.PA1, "PA1")]
+    PW = [(T.PW0, "PW0"), (T.PW1, "PW1")]
+
+    def parts(t):
+        ps, b = [], 0
+        for n, off, step in C["parts"]:
+            if t == RO - 1:
+                off, step = b, 1
+            ps.append((b, n, off, step))
+            b += n
+        return ps
+
+    def tkeys(s):
+        return OWN + ["T%d" % s]
+
+    def cols(buf, r, s, p):
+        b, n, off, step = p
+        c0 = 1024 * r + 4 * off + s
+        return buf[:, c0:c0 + 4 * step * (n - 1) + 1:4 * step]
+
+    def prep(t):
+        s = t % 4
+        tk = tkeys(s)
+        for ch, p in enumerate(parts(t)):
+            b, n = p[0], p[1]
+            h = slice(b, b + n)
+            u = cols(T.Tb, rank, s, p)
+            ts(T.ph[:, h], u, 0.0625, -2048.0, A.mult, A.add, tk, ["ph%d" % ch], n)
+            op("v", lambda q, h=h: q.transpose(T.pt[:, h], T.ph[:, h]), ["ph%d" % ch], ["pt%d" % ch], dur(n / 2))
+            nh = n // 16
+            for bb in range(n // 32):
+                for c in range(2):
+                    o = b + 2 * bb + c
+                    for gm in range(2):
+                        j = 2 * c + gm
+                        x = b + 32 * bb + 16 * gm
+                        mm(T.PX[:, o:o + 15 * nh + 1:nh], T.Pm[:, 128 * j:128 * j + 128], T.pt[:, x:x + 16], gm == 0, gm == 1,
+                           ["cPm%d" % j, "pt%d" % ch], ["PX_o"], 16)
+        ts(T.Of[:], T.PX[:, 0:256], 2048.0, None, A.add, None, ["PX_o"], ["Of"], 256)
+        for ch, p in enumerate(parts(t)):
+            b, n, off, step = p
+            h = slice(b, b + n)
+            u = cols(T.Tb, rank, s, p)
+            ts(T.zi[:, h], u, 16.0, None, A.mult, None, tk, ["zi%d" % ch], n)
+            ts(T.nm[:, h], T.zi[:, h], 4, None, A.logical_shift_right, None, ["zi%d" % ch], ["nm%d" % ch], n)
+            pa, pk = PA[(4 * b) // 512]
+            for j in range(4):
+                x = 4 * b + n * j
+                ts(T.Aq[:, x:x + n], T.zi[:, h], 1 << j, None, A.bitwise_and, None, ["zi%d" % ch], ["Aq%d%d" % (ch, j)], n)
+                ts(pa[:, x % 512:x % 512 + n], T.Aq[:, x:x + n], -1.0, float(32 + (1 << j)), A.mult, A.add,
+                   ["Aq%d%d" % (ch, j)], [pk + "%d%d" % (ch, j)], n)
+            iota(T.at[:, h], [[64 * step, n]], 16 * (1024 * rank + 4 * off + s), 0, ["at%d" % ch], n)
+        x = 128 * (t % 2)
+        ts(T.Sel[:, x:x + 128], T.pw[:], float(17 * t + 3), None, A.is_equal, None, ["pw"], ["Sel%d" % (t % 2)], 128)
+
+    def decode(s):
+        tk = tkeys(s)
+        u = T.Tb[:, 1024 * rank + s:1024 * rank + 1024:4]
+        act(T.du[:], u, F.Identity, BIG, 1.0, tk, ["du"], 256)
+        act(T.dn[:], T.du[:], F.Identity, -BIG, 1.0, ["du"], ["dn"], 256)
+        mm(T.PD0[:, 0:256], T.I16f[:], u, True, False, tk + ["I16f"], ["PD0a"], 256, True)
+        mm(T.PD0[:, 0:256], T.Im15[:], T.dn[:], False, True, ["dn", "Im15"], ["PD0a"], 256, True)
+        act(T.Yo[:, s:1024:4], T.PD0[:, 0:256], F.Identity, 0.0, 1.0, ["PD0a"], ["Y%d" % s], 256)
+
+    prep(0)
+    win_all = T.Tb[:, 0:4096]
+    TALL = OWN + ["T%d" % s for s in range(4)]
+    pdn = [0]
+    nsent = 0
+
+    for t in range(RO):
+        s = t % 4
+        last = t == RO - 1
+        ps = parts(t)
+        sel, selk = T.Sel[:, 128 * (t % 2):128 * (t % 2) + 128], "Sel%d" % (t % 2)
+        sends = []
+
+        def body(ch):
+            b, n, off, step = ps[ch]
+            h = slice(b, b + n)
+            nh = n // 16
+            c = str(ch)
+            pw_, wk = PW[ch % 2]
+            bb, bk = (T.PX, "PX_b") if ch % 2 == 0 else (T.PM, "PM_b")
+            bp = bb[:, 384:384 + n]
+
+            def gath(k, m):
+                return win_all.indirect(T.Of[:, b + nh * k:b + nh * (k + m)])
+
+            def sl(k, m=1):
+                return slice(16 * b + n * k, 16 * b + n * (k + m))
+
+            ts(T.Gb[:, h], gath(t, 1), BIG, -BIG, A.add, A.add, TALL + ["Of", "inv"], ["Gb" + c], n, True)
+            mm(bp, sel, T.Gb[:, h], True, True, [selk, "Gb" + c], [bk], n, True)
+            kk = C["vw"] // n
+            for u in range(kk):
+                o = T.Bv[:, 256 * ch + n * u:256 * ch + n * u + n]
+                if C["evs"] and ch > 0:
+                    act(o, bp, F.Identity, -OFF, 1.0, [bk], ["Bv%s%d" % (c, u)], n)
+                else:
+                    ts(o, bp, -OFF, None, A.add, None, [bk], ["Bv%s%d" % (c, u)], n)
+            nks = C["ks"][ch]
+            if nks:
+                ts(T.Bh[:, h], bp, 0.0625, -2048.0, A.mult, A.add, [bk], ["Bh" + c], n)
+            tt(T.own[:, h], T.nm[:, h], bp, A.is_equal, ["nm" + c, bk], ["own" + c], n)
+            tt(T.skp[:, h], T.at[:, h], bp, A.is_equal, ["at" + c, bk], ["skp" + c], n)
+            if not C["prep"]:
+                old, ok = oldof(ch)
+                tt(T.pre[:, h], bp, old, A.subtract, ok + [bk], ["pre" + c], n)
+            red = []
+            gs = 512 // n
+            k = 16 - nks
+            while k < 16:
+                m = min(gs, 16 - k, (nks + 1) // 2 if nks > gs else gs)
+                pb, pk = PDk[pdn[0] % 2]
+                pdn[0] += 1
+                act(T.G[:, sl(k, m)], gath(k, m), F.Identity, 0.0, 1.0, TALL + ["Of", "ins"], ["G%s_%d" % (c, k)], n * m, True)
+                for u in range(m):
+                    o = pb[:, n * u:n * u + n]
+                    mm(o, T.If[:], T.G[:, sl(k + u)], True, False, ["If", "G%s_%d" % (c, k)], [pk + "a"], n, True)
+                    mm(o, T.Ih[:], T.Bh[:, h], False, True, ["Ih", "Bh" + c], [pk + "a"], n)
+                act(T.Cl[:, sl(k, m)], pb[:, 0:n * m], F.Sigmoid, -32768.0 + OFF - 2.0, 1.0, [pk + "a"],
+                    ["Cl%s_%d" % (c, k + u) for u in range(m)], n * m)
+                red.append([(k + u, "R64") for u in range(m)])
+                k += m
+            vred = []
+            f = C["first"][ch]
+            ks = ([0] if f else []) + list(range(f, 16 - nks, kk))
+            for x, k in enumerate(ks):
+                m = (ks + [16 - nks])[x + 1] - k
+                dk = "Dv%s_%d" % (c, k)
+                tt(T.Dv[:, sl(k, m)], gath(k, m), T.Bv[:, 256 * ch:256 * ch + n * m], A.subtract,
+                   TALL + ["Of", "inv"] + ["Bv%s%d" % (c, u) for u in range(m)], [dk], n * m, True)
+                w = ["Cl%s_%d" % (c, k + u) for u in range(m)]
+                mine = x >= len(ks) - C["kc"][ch]
+                if mine:
+                    ts(T.Cl[:, sl(k, m)], T.Dv[:, sl(k, m)], 0.0, 4.0, A.max, A.min, [dk], w, n * m / 2)
+                else:
+                    act(T.Cl[:, sl(k, m)], T.Dv[:, sl(k, m)], F.Sigmoid, -2.0, 1.0, [dk], w, n * m)
+                vred.append([(k + u, "R16" if mine else "R64") for u in range(m)])
+            seq = []
+            for x in range(len(vred)):
+                seq += vred[x]
+                if x >= 1 and red:
+                    seq += red.pop(0)
+            for x in red:
+                seq += x
+            for x, (k, R) in enumerate(seq):
+                if x == len(seq) - 2:
+                    mm(pw_[:, 0:n], T.I8k[:], T.own[:, h], False, False, ["I8k", "own" + c], [wk + "w"], n)
+                mm(pw_[:, 0:n], T[R][:, 15 - k:143 - k], T.Cl[:, sl(k)], x == 0, x == len(seq) - 1,
+                   [R, "Cl%s_%d" % (c, k)], [wk + "w"], n)
+
+        def oldof(ch):
+            if last:
+                return cols(T.Yo, 0, s, ps[ch]), ["Y%d" % s]
+            return cols(T.Tb, rank, s, ps[ch]), tkeys(s)
+
+        def land(ch, r0, r1):
+            b, n = ps[ch][0], ps[ch][1]
+            x = 1024 * t + 4 * b
+            return T.L[:, x + n * r0:x + n * r1]
+
+        def tail(ch):
+            b, n, off, step = ps[ch]
+            h = slice(b, b + n)
+            c = str(ch)
+            pw_, wk = PW[ch % 2]
+            pa, pk = PA[(4 * b) // 512]
+            old, ok = oldof(ch)
+
+            def pl(buf, j, m=1):
+                return buf[:, 4 * b + n * j:4 * b + n * (j + m)]
+
+            ts(T.W[:, h], pw_[:, 0:n], 7.5, 2080.0, A.add, A.min, [wk + "w"], ["W" + c], n)
+            if C["prep"]:
+                mm(pw_[:, 128:128 + n], sel, T.Gb[:, h], True, False, [selk, "Gb" + c], [wk + "n"], n, True)
+                mm(pw_[:, 128:128 + n], T.Imf[:], old, False, False, ["Imf"] + ok, [wk + "n"], n, True)
+            for j in range(4):
+                ts(pl(T.Q, j), T.W[:, h], 32 + (1 << j), None, A.bitwise_and, None, ["W" + c], ["Q%s%d" % (c, j)], n)
+            ts(T.tes[:, h], pl(T.Q, 0), 32.0, None, A.is_ge, None, ["Q%s0" % c], ["tes" + c], n)
+            vb, vk = (T.PD0, "PD0a") if ch == NP - 1 else (T.PM, "PM_v")
+            mm(vb[0:4, 0:n], T.Vm[:, 0:4], T.tes[:, h], True, False, ["Vm", "tes" + c], [vk], n)
+            split = C["split"] and ch == NP - 1
+            xb = [(T.PX, "PX_x", 0), (T.PD1, "PD1a", 0) if split else (T.PX, "PX_x", 2 * n)]
+            for u in range(2):
+                x = (4 * b + 2 * n * u) % 512
+                tt(pl(T.E, 2 * u, 2), pl(T.Q, 2 * u, 2), pa[:, x:x + 2 * n], A.is_equal,
+                   ["Q%s%d" % (c, 2 * u + j) for j in range(2)] + [pk + "%d%d" % (ch, 2 * u + j) for j in range(2)],
+                   ["E%s%d" % (c, u)], 2 * n)
+                for j in range(2):
+                    o = xb[u][0][:, xb[u][2] + n * j:xb[u][2] + n * j + n]
+                    mm(o, T.Om[:], T.tes[:, h], True, False, ["Om", "tes" + c], [xb[u][1]], n)
+                    mm(o, T.Ob[:], pl(T.E, 2 * u + j), False, True, ["Ob", "E%s%d" % (c, u)], [xb[u][1]], n)
+            for j in range(4):
+                mm(vb[0:4, 0:n], T.Vw[:, 3 - j:7 - j], pl(T.E, j), False, j == 3, ["Vw", "E%s%d" % (c, j // 2)], [vk], n)
+            act(T.won[0:4, h], vb[0:4, 0:n], F.Sigmoid, -128.0, 256.0, [vk], ["won" + c], n)
+            if split:
+                act(pl(T.Fd, 0, 2), T.PX[:, 0:2 * n], F.Sigmoid, -49280.0, 1.0, ["PX_x"], ["Fd%s0" % c], 2 * n)
+                ts(pl(T.Fd, 2, 2), T.PD1[:, 0:2 * n], 49280.0, None, A.is_gt, None, ["PD1a"], ["Fd%s1" % c], 2 * n)
+            elif C["t4s"]:
+                act(pl(T.Fd, 0, 4), T.PX[:, 0:4 * n], F.Sigmoid, -49280.0, 1.0, ["PX_x"], ["Fd%s0" % c, "Fd%s1" % c], 4 * n)
+            else:
+                ts(pl(T.Fd, 0, 4), T.PX[:, 0:4 * n], 49280.0, None, A.is_gt, None, ["PX_x"], ["Fd%s0" % c, "Fd%s1" % c], 4 * n)
+            e = T.PM[:, 128:128 + n]
+            mm(e, T.I256[:], T.tes[:, h], True, False, ["I256", "tes" + c], ["PM_e"], n)
+            mm(e, T.I256[:], T.own[:, h], False, False, ["I256", "own" + c], ["PM_e"], n)
+            mm(e, T.Isk[:], T.skp[:, h], False, False, ["Isk", "skp" + c], ["PM_e"], n)
+            for j in range(4):
+                mm(e, T.I16[:], pl(T.E, j), False, False, ["I16", "E%s%d" % (c, j // 2)], ["PM_e"], n)
+            mm(e, T.O16[0:4, :], T.won[0:4, h], False, False, ["O16", "won" + c], ["PM_e"], n)
+            for j in range(4):
+                mm(e, T.Im32[:], pl(T.Fd, j), False, j == 3, ["Im32", "Fd%s%d" % (c, j // 2)], ["PM_e"], n)
+            x = 128 if last else 0
+            mm(pw_[:, 128:128 + n], T.Nw[0:4, x:x + 128], T.won[0:4, h], not C["prep"], True, ["Nw0", "Nw1", "won" + c], [wk + "n"], n)
+            if C["prep"]:
+                dl, dk = pw_[:, 128:128 + n], wk + "n"
+            else:
+                dl, dk = pw_[:, 256:256 + n], wk + "d"
+                tt(dl, T.pre[:, h], pw_[:, 128:128 + n], A.add, ["pre" + c, wk + "n"], [dk], n)
+            act(T.U[:, h], e, F.Sigmoid, cf(5), LN2, ["PM_e", "cf5"], ["U" + c], n)
+            mm(T.PM[:, 256:256 + n], T.Ym[:], T.U[:, h], True, True, ["Ym", "U" + c], ["PM_y"], n)
+            ts(T.win[:, h], T.PM[:, 256:256 + n], 0.0, None, A.is_lt, None, ["PM_y"], ["win" + c], n)
+            tt(pw_[:, 384:384 + n], T.win[:, h], dl, A.mult, ["win" + c, dk], [wk + "t"], n)
+            if last:
+                tt(old, old, pw_[:, 384:384 + n], A.add, ok + [wk + "t"], ["Yf" + c], n)
+                op("ys"[ch % 2], lambda q: q.dma_start(T.yk[:, 4 * b:4 * b + 4 * n], T.Yo[:, 4 * b:4 * b + 4 * n]),
+                   ["Y%d" % u for u in range(4)] + ["Yf" + c], ["out" + c], 50.0, k="d", sem="st" + c, lat=3000.0)
+                wait("ys"[ch % 2], [], [], r=["out" + c])
+            else:
+                lk = "L%d%s" % (t, c)
+                tt(land(ch, rank, rank + 1), old, pw_[:, 384:384 + n], A.add, ok + [wk + "t"], [lk], n)
+                sends.append(send(plan3, land(ch, rank, rank + 1), ["a%d_%d_%d" % (t, ch, rank)] * 3, "lsD", [lk],
+                                  C["gap"] if ch else 0.0))
+
+        def update(ch):
+            n = ps[ch][1]
+            lk = "L%d%d" % (t, ch)
+            tk = "T%d" % s
+
+            def sem(r):
+                return ("a%d_%d_%d" % (t, ch, r), len(e_near) if r == srank else hf)
+
+            if ch < NP - 1:
+                wait("s", [sem(r) for r in range(4) if r != rank], [lk + "w"], after=[(sends[ch], C["xch"]), (sends[NP - 1], 0.0)])
+                b, n, off, step = ps[ch]
+                act(T.Tb[:, 4 * off + s:4096:4 * step], land(ch, 0, 4), F.Identity, 0.0, 1.0, [lk, lk + "w", "ins"], [tk], 4 * n)
+                return
+            act(cols(T.Tb, rank, s, ps[ch]), land(ch, rank, rank + 1), F.Identity, 0.0, 1.0, [lk, "ins"], [tk], n)
+            for e, r, l in (("s", srank, C["xch"] - 1000), ("v", franks[0], C["xch"]), ("s", franks[1], C["xch"])):
+                wk = lk + "w%d" % r
+                wait(e, [sem(r)], [wk], after=[(sends[ch], l)])
+                if e == "s":
+                    act(cols(T.Tb, r, s, ps[ch]), land(ch, r, r + 1), F.Identity, 0.0, 1.0, [wk, tk], ["X%d" % r], n)
+                else:
+                    op("v", lambda q, o=cols(T.Tb, r, s, ps[ch]), i=land(ch, r, r + 1): q.tensor_copy(o, i),
+                       [wk, tk], ["X%d" % r], dur(n))
+
+        for ch in range(NP):
+            body(ch)
+            if ch > 0:
+                tail(ch - 1)
+        tail(NP - 1)
+        if not last:
+            for ch in range(NP):
+                update(ch)
+            nsent += NP * (2 * hf + len(e_near))
+            prep(t + 1)
+            if t == 0:
+                TALL = TALL + ["X%d" % r for r in range(4)]
+        if t in (1, 2, 3, 4):
+            decode(t % 4)
+    wait("g", [("lsD", nsent)], [], after=[(gq[0], 0.0)])
+    _emit(g, T, ops)

@@ -6,13 +6,16 @@ A = AluOpType
 F = ActivationFunctionType
 RO = 6
 CFG = {
-    "parts": [(128, 0, 2), (128, 1, 2)],
-    "ks": [4, 4],
-    "kc": [0, 1],
-    "vw": 256,
-    "t4s": True, "prep": True, "evs": True, "split": True, "gap": 3000.0, "jit": 300.0, "tries": 24, "merge": False, "first": [1, 1],
-    "cyc": 1.0, "pe": 0.5, "gam": 1.56, "hop": 105.0, "xch": 4300.0,
+    "parts": [(128, 0, 2), (64, 1, 2), (64, 129, 2)],
+    "ks": [6, 4, 0],
+    "kc": [0, 0, 1],
+    "vw": [256, 384],
+    "t4s": True, "prep": True, "evs": True, "split": True, "gap": 3000.0, "jit": 300.0, "tries": 1, "first": [0, 0, 0], "wins": [1, 1, 0],
+    "wide": True, "e1": [1, 0], "sc": 1,
+    "cyc": 0.85, "pe": 0.43, "ovh": 35.0, "pov": 15.0, "gam": 1.56, "hop": 105.0, "xch": 4300.0,
 }
+CFG.update({"parts": [(128, 0, 2), (128, 1, 2)], "ks": [4, 4], "kc": [0, 1], "first": [0, 0], "wins": [1, 0], "xch": 3500.0,
+            "gap": 800.0, "wide": False, "vw": [256, 256], "e1": [1, 0]})
 BIG = 1.5 * 2.0 ** 27
 OFF = 24.5 / 16.0
 LN2 = math.log(2.0)
@@ -25,10 +28,10 @@ def _sb(n, d):
 SCRATCH = {
     "Z": _sb(1024, "int32"), "Tb": _sb(4096, "float32"), "Yo": _sb(1024, "float32"), "L": _sb(5 * 1024, "float32"),
     "Dv": _sb(4096, "bfloat16"), "Cl": _sb(4096, "bfloat16"), "G": _sb(4096, "float32"),
-    "Of": _sb(256, "uint16"), "Gb": _sb(256, "float32"), "Bv": _sb(1024, "float32"), "Bh": _sb(256, "float16"),
+    "Of": _sb(256, "uint16"), "Gb": _sb(256, "float32"), "Bv": _sb(1536, "float32"), "Bh": _sb(256, "float16"),
     "own": _sb(256, "bfloat16"), "skp": _sb(256, "bfloat16"), "pre": _sb(256, "float32"), "W": _sb(256, "int32"),
     "Q": _sb(1024, "int32"), "E": _sb(1024, "bfloat16"), "tes": _sb(256, "bfloat16"), "won": _sb(256, "bfloat16"),
-    "Fd": _sb(1024, "bfloat16"), "U": _sb(256, "bfloat16"), "win": _sb(256, "float32"),
+    "Fd": _sb(1024, "bfloat16"), "U": _sb(256, "bfloat16"), "win": _sb(256, "bfloat16"),
     "zi": _sb(256, "int32"), "nm": _sb(256, "int32"), "i1": _sb(1024, "int32"), "ph": _sb(256, "float16"),
     "pt": _sb(256, "float16"), "Aq": _sb(1024, "int32"), "at": _sb(256, "float32"), "Sel": _sb(256, "float32"),
     "du": _sb(256, "float32"), "dn": _sb(256, "float32"),
@@ -45,8 +48,33 @@ for _n in ("PD0", "PD1", "PW0", "PW1", "PA0", "PA1", "PX", "PM"):
     SCRATCH[_n] = ("psum", [128, 512], "float32")
 NP = len(CFG["parts"])
 SEMAPHORES = (["ev", "es", "et", "eg", "lsI", "lsD", "arI"] + ["ld%d" % j for j in range(4)] + ["fw%d" % j for j in range(4)]
-              + ["st%d" % j for j in range(NP)]
-              + ["a%d_%d_%d" % (t, p, r) for t in range(RO - 1) for p in range(NP) for r in range(4)])
+              + ["st%d" % j for j in range(NP)] + ["h%d" % t for t in range(RO - 1)]
+              + ["a%d_%d_%d" % (t, p, r) for t in range(RO - 1) for p in range(2) for r in range(4)])
+SEED = []
+PRIO = {'sZ1': 1000, 'tPM_etes0': -150, 'vQ23': 1300, 'tPM_eE11': 600, 'tPW1wCl1_6': -1000, 'tPW0wCl2_8': 1000, 'vi12': -150,
+        'tPW0wCl0_3': 300, 'vQ12': -300, 'tPD0aG1_12': 150, 'vtes0': 150, 'vR16': -600, 'vown1': 300, 'sG1_12': -150,
+        'tPD1aBh0': 600, 'tPM_vtes1': 150, 'vL1_128': 300, 'tPM_eFd01': -600, 'tPM_yU2': 150, 'vBh0': -600, 'vAq00': -1150,
+        'vcf2': 400, 'vpt0': 300, 'tPW0wCl2_3': -300, 'tPA0n0Gb0': 600, 'vskp0': 1000, 'vFd21': 1000, 'vi11': -1000,
+        'sCl2_4': 600, 'tPD0aBh0': 1000, 'vOf': -600, 'vDv2_12': -600, 'tPW1wCl1_1': 1000, 'vAq12': -600,
+        'tPW0wCl2_9': -1000, 'vQ13': -300}
+PRIO = {'vnm1': -300, 'tPW1wCl1_5': 150, 'tPM_eFd00': -1000, 'vIm15': 600, 'tPM_vE01': -150, 'tPW0wCl0_3': -300,
+        'tPW1wCl1_9': -150, 'tPM_vtes0': -1000, 'sCl1_12': -1000, 'vIf': 150, 'tPM_eE00': -300, 'vR64': -1000,
+        'tPM_ewon1': -600, 'vI16': -600, 'vE10': 300, 'tPM_b1Gb1': -150, 'tPM_etes0': -300, 'vVm': -150, 'vci2': 300,
+        'vskp0': -600, 'vcf1': 600, 'vQ12': -1150, 'tPW0wCl0_4': -600, 'vPD1a': -1000, 'vi12': -1000, 'tPM_eskp1': 600,
+        'vPA110': 600, 'vnm0': -1000, 'vcf3': 300, 'g-': -600, 'tPD0aIm15': -150, 'gT0': -900, 'tPM_eown1': 300,
+        'gT2': -1000, 'tPW0nY1': 150, 'tPW0nNw1': -400, 'tPW0wCl0_0': -300, 'vT2': -300, 'sCl0_10': 600, 'vAq12': -600,
+        'tPM_ewon0': -600, 'vcf4': 600, 'vAq02': 300, 'tPW0nTo0': 300, 'vNw1': -150, 'vT1': -150, 'tPX_bGb0': 600,
+        'tPM_vE00': 400, 'gat0': 600, 'sFd00': -1000, 'sCl0_8': 450, 'tPM_eE01': -1000, 'tPM_yU1': 300, 'yout0': -300,
+        'tPM_eown0': 150, 'vW0': 1000, 'vDv0_2': -150, 'vwin1': -300, 'vOm': -850, 'tPD0aE10': -1000, 'tPW1wown1': 300,
+        'sdu': 300, 'tPM_eskp0': -600, 'vImf': -300, 'vPW0t': 300, 'sdn': 300, 'vtes1': 300, 'vX1': 150, 'vY': -600,
+        'sCl1_2': -1000, 'tPD1aE11': 150, 'tPW0wCl0_2': 300}
+PRIO2 = {'vAq11': 1000, 'vCl1_10': 600, 'sCl1_8': 300, 'vDv0_2': 300, 'sZ1': 600, 'tPD0aE10': -150, 'vVm': -600, 'vI16f': 150,
+        'tPM_etes0': 600, 'vNw1': -150, 'vci1': 1000, 'vI8k': 1000, 'tPM_eskp1': -300, 'tPD1ates1': 150, 'vtes1': 300,
+        'vQ10': -1600, 'tPX_xtes1': 150, 'tPW0nTo0': 300, 'tPM_eown1': 600, 'gT3': 1000, 'vE10': 300, 'vGb0': -150,
+        'vPA000': -2000, 'tPM_ewon0': -600}
+PRIO.update({'tPW1wCl1_5': 300, 'vI16': 400, 'vQ12': -150, 'tPW0nY1': -450, 'vAq02': -300, 'vDv0_4': -1000, 'vinv': -1000,
+             'vcf8': -600, 'vI256': -600, 'sCl0_4': -300, 'sCl0_6': -1000, 'vcf7': 300, 'vDv0_6': 600, 'vDv1_0': 600,
+             'vDv0_10': -600, 'tPW1nTo0': -150, 'vNw0': 600, 'vcf0': -1000, 'vVm': 0})
 ESEM = {"v": "ev", "s": "es", "t": "et", "g": "eg"}
 
 
@@ -87,6 +115,13 @@ def _deps(ops):
     return deps
 
 
+def _label(op):
+    k = (op["w"] + op["r"] + ["-"])[0]
+    if op["e"] == "t":
+        k += op["r"][1][:5]
+    return op["e"] + (k[0] + k[2:] if k[0] in "LTY" else k)
+
+
 def _order(ops, deps, seed):
     n = len(ops)
     succ = [[] for _ in range(n)]
@@ -98,6 +133,8 @@ def _order(ops, deps, seed):
     pr = [0.0] * n
     for i in range(n - 1, -1, -1):
         pr[i] = ops[i]["d"] + max([l + pr[j] for j, l in succ[i]] + [0.0])
+    for i in range(n):
+        pr[i] += PRIO.get(_label(ops[i]), 0)
     x = seed
     for i in range(n if seed else 0):
         x = (x * 1103515245 + 12345) % 2147483648
@@ -138,7 +175,9 @@ def _order(ops, deps, seed):
 def _emit(g, T, ops):
     qs = {"v": g.vector, "s": g.scalar, "t": g.tensor, "g": g, "y": g.sync}
     deps = _deps(ops)
-    order = min(_order(ops, deps, x) for x in range(CFG["tries"]))[1]
+    if not SEED:
+        SEED.append(min((_order(ops, deps, x)[0], x) for x in range(CFG["tries"]))[1])
+    order = _order(ops, deps, SEED[0])[1]
     pos = {i: p for p, i in enumerate(order)}
     seen, waits = {}, {}
     for i in order:
@@ -231,7 +270,7 @@ def rank_program(g, core, T, topo):
         return op(e, None, r, w, 0.0, k="w", sems=sems, after=after)
 
     def dur(n, gth=False):
-        return 50.0 + n * C["gam"] * C["cyc"] if gth else max(64.0, n) * C["cyc"]
+        return 50.0 + n * C["gam"] * C["cyc"] if gth else max(64.0, n) * C["cyc"] + C["ovh"]
 
     def ts(out, in0, s1, s2, o0, o1, r, w, n, gth=False):
         if s2 is None:
@@ -246,7 +285,7 @@ def rank_program(g, core, T, topo):
         op("s", lambda q: q.activation(out, in_, fn, bias=bias, scale=scale), r, w, dur(n, gth))
 
     def mm(out, lhsT, rhs, start, stop, r, w, n, f32=False):
-        op("t", lambda q: q.matmul(out, lhsT, rhs, start, stop), r, w, max(64, n) * (4 if f32 else 1) * C["pe"], lat=C["hop"] + 45)
+        op("t", lambda q: q.matmul(out, lhsT, rhs, start, stop), r, w, max(64, n) * (4 if f32 else 1) * C["pe"] + C["pov"], lat=C["hop"] + 45)
 
     def iota(out, pat, base, cm, w, n, flt=True):
         if flt:
@@ -291,7 +330,7 @@ def rank_program(g, core, T, topo):
     ts(cf(2), ci(1), 0.0, None, A.add, None, ["ci1"], ["cf2"], 1)
     ts(cf(3), ci(2), 62.5, cf(0), A.mult, A.add, ["ci2", "cf0"], ["cf3"], 1)
     ts(cf(4), ci(2), -62.5, cf(0), A.mult, A.add, ["ci2", "cf0"], ["cf4"], 1)
-    ts(cf(5), ci(3), -LN2, -LN2 * 336.0, A.mult, A.add, ["ci3"], ["cf5"], 1)
+    ts(cf(5), ci(3), -LN2, -LN2 * 330.0, A.mult, A.add, ["ci3"], ["cf5"], 1)
     ts(cf(6), ci(5), 1.5, 1.0, A.mult, A.add, ["ci5"], ["cf6"], 1)
     ts(cf(7), ci(4), 1.0, cf(6), A.add, A.mult, ["ci4", "cf6"], ["cf7"], 1)
     ts(cf(8), cf(7), 0.0625, None, A.mult, None, ["cf7"], ["cf8"], 1)
@@ -378,14 +417,15 @@ def rank_program(g, core, T, topo):
             b, n, off, step = p
             h = slice(b, b + n)
             u = cols(T.Tb, rank, s, p)
-            ts(T.zi[:, h], u, 16.0, None, A.mult, None, tk, ["zi%d" % ch], n)
-            ts(T.nm[:, h], T.zi[:, h], 4, None, A.logical_shift_right, None, ["zi%d" % ch], ["nm%d" % ch], n)
+            ts(T.zi[:, h], u, -16.0, 1048575.0, A.mult, A.add, tk, ["zi%d" % ch], n)
+            ts(T.nm[:, h], u, BIG, -BIG, A.add, A.add, tk, ["nm%d" % ch], n)
             pa, pk = PA[(4 * b) // 512]
             for j in range(4):
                 x = 4 * b + n * j
-                ts(T.Aq[:, x:x + n], T.zi[:, h], 1 << j, None, A.bitwise_and, None, ["zi%d" % ch], ["Aq%d%d" % (ch, j)], n)
-                ts(pa[:, x % 512:x % 512 + n], T.Aq[:, x:x + n], -1.0, float(32 + (1 << j)), A.mult, A.add,
-                   ["Aq%d%d" % (ch, j)], [pk + "%d%d" % (ch, j)], n)
+                ts(T.Aq[:, x:x + n], T.zi[:, h], 32 + (1 << j), None, A.bitwise_and, None, ["zi%d" % ch], ["Aq%d%d" % (ch, j)], n)
+            op("v", lambda q, o=pa[:, 4 * b % 512:4 * b % 512 + 4 * n], i=T.Aq[:, 4 * b:4 * b + 4 * n]: q.tensor_copy(o, i),
+               ["Aq%d%d" % (ch, j) for j in range(4)], [pk + "%d%d" % (ch, j) for j in range(4)]
+               + (["PA0%s%d" % (u, v) for u in "nt" for v in range(NP)] if ch == 0 else []), dur(4 * n))
             iota(T.at[:, h], [[64 * step, n]], 16 * (1024 * rank + 4 * off + s), 0, ["at%d" % ch], n)
         x = 128 * (t % 2)
         ts(T.Sel[:, x:x + 128], T.pw[:], float(17 * t + 3), None, A.is_equal, None, ["pw"], ["Sel%d" % (t % 2)], 128)
@@ -412,14 +452,48 @@ def rank_program(g, core, T, topo):
         sel, selk = T.Sel[:, 128 * (t % 2):128 * (t % 2) + 128], "Sel%d" % (t % 2)
         sends = []
 
+        def bcast(ch):
+            b, n = ps[ch][0], ps[ch][1]
+            bp, bk = (T.PX[:, 384:384 + n], "PX_b") if ch == 0 else (T.PM[:, 256 + b:256 + b + n], "PM_b%d" % ch)
+            if C["wide"]:
+                bp, bk = T.PX[:, 256 + b:256 + b + n], "PX_b%d" % ch
+            nh = n // 16
+            ts(T.Gb[:, b:b + n], win_all.indirect(T.Of[:, b + nh * t:b + nh * (t + 1)]), BIG, -BIG, A.add, A.add,
+               TALL + ["Of", "inv"], ["Gb%d" % ch], n, True)
+            mm(bp, sel, T.Gb[:, b:b + n], True, True, [selk, "Gb%d" % ch], [bk], n, True)
+            return bp, bk
+
+        def head(ch, bp, bk):
+            b, n, off, step = ps[ch]
+            h = slice(b, b + n)
+            c = str(ch)
+            for u in range(C["vw"][ch] // n):
+                o = T.Bv[:, 512 * ch + n * u:512 * ch + n * u + n]
+                if C["evs"] and ch > 0:
+                    act(o, bp, F.Identity, -OFF, 1.0, [bk], ["Bv%s%d" % (c, u)], n)
+                else:
+                    ts(o, bp, -OFF, None, A.add, None, [bk], ["Bv%s%d" % (c, u)], n)
+            if C["wide"]:
+                if ch == 0:
+                    bp, al = T.PX[:, 256:512], [str(x) for x in range(NP)]
+                    bk = ["PX_b" + x for x in al]
+                    ts(T.Bh[:], bp, 0.0625, -2048.0, A.mult, A.add, bk, ["Bh" + x for x in al], 256)
+                    tt(T.own[:], T.nm[:], bp, A.is_equal, ["nm" + x for x in al] + bk, ["own" + x for x in al], 256)
+                    tt(T.skp[:], T.at[:], bp, A.is_equal, ["at" + x for x in al] + bk, ["skp" + x for x in al], 256)
+                return
+            if C["ks"][ch]:
+                ts(T.Bh[:, h], bp, 0.0625, -2048.0, A.mult, A.add, [bk], ["Bh" + c], n)
+            tt(T.own[:, h], T.nm[:, h], bp, A.is_equal, ["nm" + c, bk], ["own" + c], n)
+            tt(T.skp[:, h], T.at[:, h], bp, A.is_equal, ["at" + c, bk], ["skp" + c], n)
+
         def body(ch):
             b, n, off, step = ps[ch]
             h = slice(b, b + n)
             nh = n // 16
             c = str(ch)
             pw_, wk = PW[ch % 2]
-            bb, bk = (T.PX, "PX_b") if ch % 2 == 0 else (T.PM, "PM_b")
-            bp = bb[:, 384:384 + n]
+            kk = C["vw"][ch] // n
+            nks = C["ks"][ch]
 
             def gath(k, m):
                 return win_all.indirect(T.Of[:, b + nh * k:b + nh * (k + m)])
@@ -427,23 +501,6 @@ def rank_program(g, core, T, topo):
             def sl(k, m=1):
                 return slice(16 * b + n * k, 16 * b + n * (k + m))
 
-            ts(T.Gb[:, h], gath(t, 1), BIG, -BIG, A.add, A.add, TALL + ["Of", "inv"], ["Gb" + c], n, True)
-            mm(bp, sel, T.Gb[:, h], True, True, [selk, "Gb" + c], [bk], n, True)
-            kk = C["vw"] // n
-            for u in range(kk):
-                o = T.Bv[:, 256 * ch + n * u:256 * ch + n * u + n]
-                if C["evs"] and ch > 0:
-                    act(o, bp, F.Identity, -OFF, 1.0, [bk], ["Bv%s%d" % (c, u)], n)
-                else:
-                    ts(o, bp, -OFF, None, A.add, None, [bk], ["Bv%s%d" % (c, u)], n)
-            nks = C["ks"][ch]
-            if nks:
-                ts(T.Bh[:, h], bp, 0.0625, -2048.0, A.mult, A.add, [bk], ["Bh" + c], n)
-            tt(T.own[:, h], T.nm[:, h], bp, A.is_equal, ["nm" + c, bk], ["own" + c], n)
-            tt(T.skp[:, h], T.at[:, h], bp, A.is_equal, ["at" + c, bk], ["skp" + c], n)
-            if not C["prep"]:
-                old, ok = oldof(ch)
-                tt(T.pre[:, h], bp, old, A.subtract, ok + [bk], ["pre" + c], n)
             red = []
             gs = 512 // n
             k = 16 - nks
@@ -452,10 +509,9 @@ def rank_program(g, core, T, topo):
                 pb, pk = PDk[pdn[0] % 2]
                 pdn[0] += 1
                 act(T.G[:, sl(k, m)], gath(k, m), F.Identity, 0.0, 1.0, TALL + ["Of", "ins"], ["G%s_%d" % (c, k)], n * m, True)
+                mm(pb[:, 0:n * m], T.If[:], T.G[:, sl(k, m)], True, False, ["If", "G%s_%d" % (c, k)], [pk + "a"], n * m, True)
                 for u in range(m):
-                    o = pb[:, n * u:n * u + n]
-                    mm(o, T.If[:], T.G[:, sl(k + u)], True, False, ["If", "G%s_%d" % (c, k)], [pk + "a"], n, True)
-                    mm(o, T.Ih[:], T.Bh[:, h], False, True, ["Ih", "Bh" + c], [pk + "a"], n)
+                    mm(pb[:, n * u:n * u + n], T.Ih[:], T.Bh[:, h], False, u == m - 1, ["Ih", "Bh" + c], [pk + "a"], n)
                 act(T.Cl[:, sl(k, m)], pb[:, 0:n * m], F.Sigmoid, -32768.0 + OFF - 2.0, 1.0, [pk + "a"],
                     ["Cl%s_%d" % (c, k + u) for u in range(m)], n * m)
                 red.append([(k + u, "R64") for u in range(m)])
@@ -466,7 +522,7 @@ def rank_program(g, core, T, topo):
             for x, k in enumerate(ks):
                 m = (ks + [16 - nks])[x + 1] - k
                 dk = "Dv%s_%d" % (c, k)
-                tt(T.Dv[:, sl(k, m)], gath(k, m), T.Bv[:, 256 * ch:256 * ch + n * m], A.subtract,
+                tt(T.Dv[:, sl(k, m)], gath(k, m), T.Bv[:, 512 * ch:512 * ch + n * m], A.subtract,
                    TALL + ["Of", "inv"] + ["Bv%s%d" % (c, u) for u in range(m)], [dk], n * m, True)
                 w = ["Cl%s_%d" % (c, k + u) for u in range(m)]
                 mine = x >= len(ks) - C["kc"][ch]
@@ -493,10 +549,9 @@ def rank_program(g, core, T, topo):
                 return cols(T.Yo, 0, s, ps[ch]), ["Y%d" % s]
             return cols(T.Tb, rank, s, ps[ch]), tkeys(s)
 
-        def land(ch, r0, r1):
-            b, n = ps[ch][0], ps[ch][1]
-            x = 1024 * t + 4 * b
-            return T.L[:, x + n * r0:x + n * r1]
+        def land(gr, r0, r1):
+            x = 1024 * t + 512 * gr
+            return T.L[:, x + 128 * r0:x + 128 * r1]
 
         def tail(ch):
             b, n, off, step = ps[ch]
@@ -510,9 +565,6 @@ def rank_program(g, core, T, topo):
                 return buf[:, 4 * b + n * j:4 * b + n * (j + m)]
 
             ts(T.W[:, h], pw_[:, 0:n], 7.5, 2080.0, A.add, A.min, [wk + "w"], ["W" + c], n)
-            if C["prep"]:
-                mm(pw_[:, 128:128 + n], sel, T.Gb[:, h], True, False, [selk, "Gb" + c], [wk + "n"], n, True)
-                mm(pw_[:, 128:128 + n], T.Imf[:], old, False, False, ["Imf"] + ok, [wk + "n"], n, True)
             for j in range(4):
                 ts(pl(T.Q, j), T.W[:, h], 32 + (1 << j), None, A.bitwise_and, None, ["W" + c], ["Q%s%d" % (c, j)], n)
             ts(T.tes[:, h], pl(T.Q, 0), 32.0, None, A.is_ge, None, ["Q%s0" % c], ["tes" + c], n)
@@ -522,16 +574,27 @@ def rank_program(g, core, T, topo):
             xb = [(T.PX, "PX_x", 0), (T.PD1, "PD1a", 0) if split else (T.PX, "PX_x", 2 * n)]
             for u in range(2):
                 x = (4 * b + 2 * n * u) % 512
-                tt(pl(T.E, 2 * u, 2), pl(T.Q, 2 * u, 2), pa[:, x:x + 2 * n], A.is_equal,
-                   ["Q%s%d" % (c, 2 * u + j) for j in range(2)] + [pk + "%d%d" % (ch, 2 * u + j) for j in range(2)],
-                   ["E%s%d" % (c, u)], 2 * n)
+                if not C["e1"][ch]:
+                    tt(pl(T.E, 2 * u, 2), pl(T.Q, 2 * u, 2), pa[:, x:x + 2 * n], A.is_equal,
+                       ["Q%s%d" % (c, 2 * u + j) for j in range(2)] + [pk + "%d%d" % (ch, 2 * u + j) for j in range(2)],
+                       ["E%s%d" % (c, u)], 2 * n)
+                elif u == 0:
+                    tt(pl(T.E, 0, 4), pl(T.Q, 0, 4), pa[:, x:x + 4 * n], A.is_equal,
+                       ["Q%s%d" % (c, j) for j in range(4)] + [pk + "%d%d" % (ch, j) for j in range(4)],
+                       ["E%s0" % c, "E%s1" % c], 4 * n)
                 for j in range(2):
                     o = xb[u][0][:, xb[u][2] + n * j:xb[u][2] + n * j + n]
                     mm(o, T.Om[:], T.tes[:, h], True, False, ["Om", "tes" + c], [xb[u][1]], n)
                     mm(o, T.Ob[:], pl(T.E, 2 * u + j), False, True, ["Ob", "E%s%d" % (c, u)], [xb[u][1]], n)
+            if NP == 2:
+                dl, dk, td, tk = pw_[:, 128:128 + n], wk + "n", pw_[:, 384:384 + n], wk + "t"
+            else:
+                dl, dk, td, tk = T.PA0[:, b:b + n], "PA0n" + c, T.PA0[:, 256 + b:256 + b + n], "PA0t" + c
             for j in range(4):
                 mm(vb[0:4, 0:n], T.Vw[:, 3 - j:7 - j], pl(T.E, j), False, j == 3, ["Vw", "E%s%d" % (c, j // 2)], [vk], n)
             act(T.won[0:4, h], vb[0:4, 0:n], F.Sigmoid, -128.0, 256.0, [vk], ["won" + c], n)
+            mm(dl, sel, T.Gb[:, h], True, False, [selk, "Gb" + c], [dk], n, True)
+            mm(dl, T.Imf[:], old, False, False, ["Imf"] + ok, [dk], n, True)
             if split:
                 act(pl(T.Fd, 0, 2), T.PX[:, 0:2 * n], F.Sigmoid, -49280.0, 1.0, ["PX_x"], ["Fd%s0" % c], 2 * n)
                 ts(pl(T.Fd, 2, 2), T.PD1[:, 0:2 * n], 49280.0, None, A.is_gt, None, ["PD1a"], ["Fd%s1" % c], 2 * n)
@@ -549,59 +612,65 @@ def rank_program(g, core, T, topo):
             for j in range(4):
                 mm(e, T.Im32[:], pl(T.Fd, j), False, j == 3, ["Im32", "Fd%s%d" % (c, j // 2)], ["PM_e"], n)
             x = 128 if last else 0
-            mm(pw_[:, 128:128 + n], T.Nw[0:4, x:x + 128], T.won[0:4, h], not C["prep"], True, ["Nw0", "Nw1", "won" + c], [wk + "n"], n)
-            if C["prep"]:
-                dl, dk = pw_[:, 128:128 + n], wk + "n"
-            else:
-                dl, dk = pw_[:, 256:256 + n], wk + "d"
-                tt(dl, T.pre[:, h], pw_[:, 128:128 + n], A.add, ["pre" + c, wk + "n"], [dk], n)
+            mm(dl, T.Nw[0:4, x:x + 128], T.won[0:4, h], False, True, ["Nw0", "Nw1", "won" + c], [dk], n)
             act(T.U[:, h], e, F.Sigmoid, cf(5), LN2, ["PM_e", "cf5"], ["U" + c], n)
             mm(T.PM[:, 256:256 + n], T.Ym[:], T.U[:, h], True, True, ["Ym", "U" + c], ["PM_y"], n)
-            ts(T.win[:, h], T.PM[:, 256:256 + n], 0.0, None, A.is_lt, None, ["PM_y"], ["win" + c], n)
-            tt(pw_[:, 384:384 + n], T.win[:, h], dl, A.mult, ["win" + c, dk], [wk + "t"], n)
+            if C["wins"][ch]:
+                act(T.win[:, h], T.PM[:, 256:256 + n], F.Sigmoid, -115.0, -9.0e28, ["PM_y"], ["win" + c], n)
+            else:
+                ts(T.win[:, h], T.PM[:, 256:256 + n], 0.0, None, A.is_lt, None, ["PM_y"], ["win" + c], n)
+            tt(td, T.win[:, h], dl, A.mult, ["win" + c, dk], [tk], n)
             if last:
-                tt(old, old, pw_[:, 384:384 + n], A.add, ok + [wk + "t"], ["Yf" + c], n)
+                tt(old, old, td, A.add, ok + [tk], ["Yf" + c], n)
                 op("ys"[ch % 2], lambda q: q.dma_start(T.yk[:, 4 * b:4 * b + 4 * n], T.Yo[:, 4 * b:4 * b + 4 * n]),
                    ["Y%d" % u for u in range(4)] + ["Yf" + c], ["out" + c], 50.0, k="d", sem="st" + c, lat=3000.0)
                 wait("ys"[ch % 2], [], [], r=["out" + c])
             else:
-                lk = "L%d%s" % (t, c)
-                tt(land(ch, rank, rank + 1), old, pw_[:, 384:384 + n], A.add, ok + [wk + "t"], [lk], n)
-                sends.append(send(plan3, land(ch, rank, rank + 1), ["a%d_%d_%d" % (t, ch, rank)] * 3, "lsD", [lk],
-                                  C["gap"] if ch else 0.0))
+                gr = b // 128
+                x = 1024 * t + 512 * gr + 128 * rank + b % 128
+                tt(T.L[:, x:x + n], old, td, A.add, ok + [tk], ["L%d%d_%d" % (t, gr, b)], n)
+                if (b + n) % 128 == 0:
+                    sends.append(send(plan3, land(gr, rank, rank + 1), ["a%d_%d_%d" % (t, gr, rank)] * 3, "lsD", lkeys(gr),
+                                      C["gap"] if gr else 0.0))
+
+        def lkeys(gr):
+            return ["L%d%d_%d" % (t, gr, p[0]) for p in ps if p[0] // 128 == gr]
 
         def update(ch):
-            n = ps[ch][1]
+            n = 128
             lk = "L%d%d" % (t, ch)
             tk = "T%d" % s
+            pg = (128 * ch, 128, ch, 2)
 
             def sem(r):
                 return ("a%d_%d_%d" % (t, ch, r), len(e_near) if r == srank else hf)
 
-            if ch < NP - 1:
-                wait("s", [sem(r) for r in range(4) if r != rank], [lk + "w"], after=[(sends[ch], C["xch"]), (sends[NP - 1], 0.0)])
-                b, n, off, step = ps[ch]
-                act(T.Tb[:, 4 * off + s:4096:4 * step], land(ch, 0, 4), F.Identity, 0.0, 1.0, [lk, lk + "w", "ins"], [tk], 4 * n)
+            if ch == 0:
+                wait("s", [sem(r) for r in range(4) if r != rank], [lk + "w"], after=[(sends[0], C["xch"]), (sends[1], 0.0)])
+                act(T.Tb[:, s:4096:8], land(0, 0, 4), F.Identity, 0.0, 1.0, lkeys(0) + [lk + "w", "ins"], [tk], 4 * n)
                 return
-            act(cols(T.Tb, rank, s, ps[ch]), land(ch, rank, rank + 1), F.Identity, 0.0, 1.0, [lk, "ins"], [tk], n)
+            act(cols(T.Tb, rank, s, pg), land(ch, rank, rank + 1), F.Identity, 0.0, 1.0, lkeys(1) + ["ins"], [tk], n)
             for e, r, l in (("s", srank, C["xch"] - 1000), ("v", franks[0], C["xch"]), ("s", franks[1], C["xch"])):
                 wk = lk + "w%d" % r
                 wait(e, [sem(r)], [wk], after=[(sends[ch], l)])
                 if e == "s":
-                    act(cols(T.Tb, r, s, ps[ch]), land(ch, r, r + 1), F.Identity, 0.0, 1.0, [wk, tk], ["X%d" % r], n)
+                    act(cols(T.Tb, r, s, pg), land(ch, r, r + 1), F.Identity, 0.0, 1.0, [wk, tk], ["X%d" % r], n)
                 else:
-                    op("v", lambda q, o=cols(T.Tb, r, s, ps[ch]), i=land(ch, r, r + 1): q.tensor_copy(o, i),
+                    op("v", lambda q, o=cols(T.Tb, r, s, pg), i=land(ch, r, r + 1): q.tensor_copy(o, i),
                        [wk, tk], ["X%d" % r], dur(n))
 
+        bs = [bcast(ch) for ch in range(NP)]
+        for ch in range(NP):
+            head(ch, *bs[ch])
         for ch in range(NP):
             body(ch)
             if ch > 0:
                 tail(ch - 1)
         tail(NP - 1)
         if not last:
-            for ch in range(NP):
+            for ch in range(2):
                 update(ch)
-            nsent += NP * (2 * hf + len(e_near))
+            nsent += 2 * (2 * hf + len(e_near))
             prep(t + 1)
             if t == 0:
                 TALL = TALL + ["X%d" % r for r in range(4)]

@@ -6,17 +6,31 @@ A = AluOpType
 F = ActivationFunctionType
 RO = 6
 CFG = {
-    "parts": [(128, 0, 2), (64, 1, 2), (64, 129, 2)],
-    "ks": [6, 4, 0],
-    "kc": [0, 0, 1],
-    "vw": [256, 384],
-    "t4s": True, "prep": True, "evs": True, "split": True, "gap": 3000.0, "jit": 300.0, "tries": 1, "first": [0, 0, 0], "wins": [1, 1, 0],
-    "wide": True, "e1": [1, 0], "sc": 1,
-    "cyc": 0.85, "pe": 0.43, "ovh": 35.0, "pov": 15.0, "gam": 1.56, "hop": 105.0, "xch": 4300.0,
+    "parts": [128, 128],
+    "ks": [5, 5],
+    "kc": [1, 1],
+    "vw": [256, 256],
+    "sw": [384, 384],
+    "bvs": "vs",
+    "wins": "sv",
+    "fds": ["s", "sv"],
+    "e1": [1, 0],
+    "xs": [1, 0],
+    "cuts": [0, 128, 256],
+    "gap": 800.0, "xch": 3500.0, "low": 0.0,
+    "cyc": 0.83, "pe": 0.42, "ovh": 30.0, "pov": 10.0, "gam": 1.56, "hop": 60.0,
 }
-CFG.update({"parts": [(128, 0, 2), (128, 1, 2)], "ks": [4, 4], "kc": [0, 1], "first": [0, 0], "wins": [1, 0], "xch": 3500.0,
-            "gap": 800.0, "wide": False, "vw": [256, 256], "e1": [1, 0]})
+PRIO = {}
+CFG.update({"ks": [5, 4], "kc": [0, 1], "sw": [384, 256], "xch": 3200.0})
+ORDER = [
+    ("v", "Gb0 Gb1 Bv0 own0 Dv0_0 Dv0_2 Dv0_4 Dv0_6 Dv0_8 Dv0_10 Dv1_0 own1 Dv1_2 W0 Dv1_4 Q00 Q01 Q02 Q03 tes0 E00 "
+          "Dv1_6 Dv1_8 Dv1_10 Cl1_10 W1 Q10 Q11 tes1 E10 Q12 Q13 E11 PW0t L0 f0 Fd11 nm win1 PW1t L1 f1 ph pt Sel cs Sv"),
+    ("s", "G0_14 G0_11 Cl0_0 Bv1 Cl0_2 Cl0_4 Cl0_11 Cl0_6 Cl0_8 Cl0_14 Cl0_10 G1_12 Cl1_0 G1_14 Cl1_12 Cl1_2 Cl1_4 Cl1_14 "
+          "Cl1_6 won0 Cl1_8 Fd00 U0 win0 Fd10 won1 U1 H00"),
+    ("t", "PX_eyU1 PD0aTo1"), ("t", "PX_eyU1 PA000Cr00"), ("t", "PX_eyU1 PA110Cr10"),
+]
 BIG = 1.5 * 2.0 ** 27
+MID = 32768.0
 OFF = 24.5 / 16.0
 LN2 = math.log(2.0)
 
@@ -28,53 +42,29 @@ def _sb(n, d):
 SCRATCH = {
     "Z": _sb(1024, "int32"), "Tb": _sb(4096, "float32"), "Yo": _sb(1024, "float32"), "L": _sb(5 * 1024, "float32"),
     "Dv": _sb(4096, "bfloat16"), "Cl": _sb(4096, "bfloat16"), "G": _sb(4096, "float32"),
-    "Of": _sb(256, "uint16"), "Gb": _sb(256, "float32"), "Bv": _sb(1536, "float32"), "Bh": _sb(256, "float16"),
-    "own": _sb(256, "bfloat16"), "skp": _sb(256, "bfloat16"), "pre": _sb(256, "float32"), "W": _sb(256, "int32"),
+    "Of": _sb(256, "uint16"), "Gb": _sb(256, "float16"), "Bv": _sb(1536, "float32"),
+    "own": _sb(256, "bfloat16"), "W": _sb(256, "int32"),
     "Q": _sb(1024, "int32"), "E": _sb(1024, "bfloat16"), "tes": _sb(256, "bfloat16"), "won": _sb(256, "bfloat16"),
     "Fd": _sb(1024, "bfloat16"), "U": _sb(256, "bfloat16"), "win": _sb(256, "bfloat16"),
-    "zi": _sb(256, "int32"), "nm": _sb(256, "int32"), "i1": _sb(1024, "int32"), "ph": _sb(256, "float16"),
-    "pt": _sb(256, "float16"), "Aq": _sb(1024, "int32"), "at": _sb(256, "float32"), "Sel": _sb(256, "float32"),
-    "du": _sb(256, "float32"), "dn": _sb(256, "float32"),
-    "xc": _sb(144, "float32"), "xg": _sb(128, "float32"), "pw": _sb(128, "float32"), "ci": _sb(16, "int32"),
-    "cf": _sb(16, "float32"), "R64": _sb(144, "bfloat16"), "R16": _sb(144, "bfloat16"),
-    "If": _sb(128, "float32"), "Imf": _sb(128, "float32"), "I16f": _sb(128, "float32"), "Im15": _sb(128, "float32"),
-    "Ih": _sb(128, "float16"), "Im32": _sb(128, "bfloat16"), "I16": _sb(128, "bfloat16"), "I256": _sb(128, "bfloat16"),
-    "I8k": _sb(128, "bfloat16"), "Isk": _sb(128, "bfloat16"), "Ym": _sb(128, "bfloat16"),
-    "c1": _sb(128, "float32"), "c2": _sb(128, "float32"), "Pm": _sb(512, "float16"),
-    "Om": _sb(128, "bfloat16"), "Ob": _sb(128, "bfloat16"), "O16": _sb(128, "bfloat16"),
-    "Nw": _sb(256, "bfloat16"), "Vw": _sb(16, "bfloat16"), "Vm": _sb(16, "bfloat16"),
+    "nm": _sb(256, "float16"), "Im1h": _sb(128, "float16"), "Ims": _sb(128, "bfloat16"), "Bw": _sb(512, "bfloat16"), "i1": _sb(1024, "int32"), "ph": _sb(256, "float16"),
+    "pt": _sb(256, "float16"), "H": _sb(1024, "bfloat16"), "Sel": _sb(128 * RO, "float16"), "Sv": _sb(8 * RO, "float16"),
+    "dn": _sb(256, "float16"),
+    "xc": _sb(256, "float32"), "xg": _sb(128, "float32"), "pw": _sb(128, "float32"), "ci": _sb(16, "int32"),
+    "cf": _sb(32, "float32"), "R64": _sb(144, "bfloat16"), "R16": _sb(144, "bfloat16"),
+    "Imf": _sb(128, "float32"), "I16f": _sb(128, "float32"), "Im15": _sb(128, "float16"), "Im16": _sb(128, "float16"),
+    "Im32": _sb(128, "bfloat16"), "I16": _sb(128, "bfloat16"), "I256": _sb(128, "bfloat16"),
+    "I8k": _sb(128, "bfloat16"), "I1": _sb(128, "bfloat16"), "Im1": _sb(128, "bfloat16"), "Ym": _sb(128, "bfloat16"),
+    "c2": _sb(128, "bfloat16"), "Pm": _sb(512, "float16"),
+    "Om": _sb(128, "bfloat16"), "Ob": _sb(128, "bfloat16"), "O16": _sb(128, "bfloat16"), "O1": _sb(128, "bfloat16"),
+    "Osk": _sb(128, "bfloat16"),
+    "Nw": _sb(256, "bfloat16"), "Vw": _sb(16, "bfloat16"), "Vm": _sb(8, "bfloat16"), "vr": _sb(8, "float32"),
+    "Iv": _sb(8, "bfloat16"), "xi": _sb(256, "bfloat16"), "Cr": _sb(1024, "bfloat16"),
 }
 for _n in ("PD0", "PD1", "PW0", "PW1", "PA0", "PA1", "PX", "PM"):
     SCRATCH[_n] = ("psum", [128, 512], "float32")
-NP = len(CFG["parts"])
 SEMAPHORES = (["ev", "es", "et", "eg", "lsI", "lsD", "arI"] + ["ld%d" % j for j in range(4)] + ["fw%d" % j for j in range(4)]
-              + ["st%d" % j for j in range(NP)] + ["h%d" % t for t in range(RO - 1)]
-              + ["a%d_%d_%d" % (t, p, r) for t in range(RO - 1) for p in range(2) for r in range(4)])
-SEED = []
-PRIO = {'sZ1': 1000, 'tPM_etes0': -150, 'vQ23': 1300, 'tPM_eE11': 600, 'tPW1wCl1_6': -1000, 'tPW0wCl2_8': 1000, 'vi12': -150,
-        'tPW0wCl0_3': 300, 'vQ12': -300, 'tPD0aG1_12': 150, 'vtes0': 150, 'vR16': -600, 'vown1': 300, 'sG1_12': -150,
-        'tPD1aBh0': 600, 'tPM_vtes1': 150, 'vL1_128': 300, 'tPM_eFd01': -600, 'tPM_yU2': 150, 'vBh0': -600, 'vAq00': -1150,
-        'vcf2': 400, 'vpt0': 300, 'tPW0wCl2_3': -300, 'tPA0n0Gb0': 600, 'vskp0': 1000, 'vFd21': 1000, 'vi11': -1000,
-        'sCl2_4': 600, 'tPD0aBh0': 1000, 'vOf': -600, 'vDv2_12': -600, 'tPW1wCl1_1': 1000, 'vAq12': -600,
-        'tPW0wCl2_9': -1000, 'vQ13': -300}
-PRIO = {'vnm1': -300, 'tPW1wCl1_5': 150, 'tPM_eFd00': -1000, 'vIm15': 600, 'tPM_vE01': -150, 'tPW0wCl0_3': -300,
-        'tPW1wCl1_9': -150, 'tPM_vtes0': -1000, 'sCl1_12': -1000, 'vIf': 150, 'tPM_eE00': -300, 'vR64': -1000,
-        'tPM_ewon1': -600, 'vI16': -600, 'vE10': 300, 'tPM_b1Gb1': -150, 'tPM_etes0': -300, 'vVm': -150, 'vci2': 300,
-        'vskp0': -600, 'vcf1': 600, 'vQ12': -1150, 'tPW0wCl0_4': -600, 'vPD1a': -1000, 'vi12': -1000, 'tPM_eskp1': 600,
-        'vPA110': 600, 'vnm0': -1000, 'vcf3': 300, 'g-': -600, 'tPD0aIm15': -150, 'gT0': -900, 'tPM_eown1': 300,
-        'gT2': -1000, 'tPW0nY1': 150, 'tPW0nNw1': -400, 'tPW0wCl0_0': -300, 'vT2': -300, 'sCl0_10': 600, 'vAq12': -600,
-        'tPM_ewon0': -600, 'vcf4': 600, 'vAq02': 300, 'tPW0nTo0': 300, 'vNw1': -150, 'vT1': -150, 'tPX_bGb0': 600,
-        'tPM_vE00': 400, 'gat0': 600, 'sFd00': -1000, 'sCl0_8': 450, 'tPM_eE01': -1000, 'tPM_yU1': 300, 'yout0': -300,
-        'tPM_eown0': 150, 'vW0': 1000, 'vDv0_2': -150, 'vwin1': -300, 'vOm': -850, 'tPD0aE10': -1000, 'tPW1wown1': 300,
-        'sdu': 300, 'tPM_eskp0': -600, 'vImf': -300, 'vPW0t': 300, 'sdn': 300, 'vtes1': 300, 'vX1': 150, 'vY': -600,
-        'sCl1_2': -1000, 'tPD1aE11': 150, 'tPW0wCl0_2': 300}
-PRIO2 = {'vAq11': 1000, 'vCl1_10': 600, 'sCl1_8': 300, 'vDv0_2': 300, 'sZ1': 600, 'tPD0aE10': -150, 'vVm': -600, 'vI16f': 150,
-        'tPM_etes0': 600, 'vNw1': -150, 'vci1': 1000, 'vI8k': 1000, 'tPM_eskp1': -300, 'tPD1ates1': 150, 'vtes1': 300,
-        'vQ10': -1600, 'tPX_xtes1': 150, 'tPW0nTo0': 300, 'tPM_eown1': 600, 'gT3': 1000, 'vE10': 300, 'vGb0': -150,
-        'vPA000': -2000, 'tPM_ewon0': -600}
-PRIO.update({'tPW1wCl1_5': 300, 'vI16': 400, 'vQ12': -150, 'tPW0nY1': -450, 'vAq02': -300, 'vDv0_4': -1000, 'vinv': -1000,
-             'vcf8': -600, 'vI256': -600, 'sCl0_4': -300, 'sCl0_6': -1000, 'vcf7': 300, 'vDv0_6': 600, 'vDv1_0': 600,
-             'vDv0_10': -600, 'tPW1nTo0': -150, 'vNw0': 600, 'vcf0': -1000, 'vVm': 0})
+              + ["st%d" % j for j in range(4)]
+              + ["a%d_%d_%d" % (t, p, r) for t in range(RO - 1) for p in range(4) for r in range(4)])
 ESEM = {"v": "ev", "s": "es", "t": "et", "g": "eg"}
 
 
@@ -86,30 +76,38 @@ def _mask(engines):
 
 
 def _deps(ops):
-    lastw, readers, bank, deps = {}, {}, {}, []
+    lastw, readers, bank, deps, before = {}, {}, {}, [], {}
     for n, op in enumerate(ops):
         d = set()
         for k in op["r"]:
-            if k in lastw:
-                d.add(lastw[k])
-        for k in op["w"]:
-            if k in lastw:
-                d.add(lastw[k])
-            d.update(readers.get(k, []))
-        for k in set(k[:3] for k in op["r"] + op["w"] if k[0] == "P"):
-            b = bank.setdefault(k, [None, [], []])
-            if b[0] != op["e"]:
-                b[0], b[1], b[2] = op["e"], [], b[1]
-            d.update(b[2])
-            if op["e"] == "t" and b[1]:
-                d.add(b[1][-1])
-            b[1].append(n)
+            d.update(lastw.get(k, []))
+        grp = op.get("grp")
+        if grp in before:
+            d.update(before[grp])
+            lastw[op["w"][0]].append(n)
+            bank[op["w"][0][:3]][1].append(n)
+        else:
+            e = set()
+            for k in op["w"]:
+                e.update(lastw.get(k, []))
+                e.update(readers.get(k, []))
+            for k in set(k[:3] for k in op["r"] + op["w"] if k[0] == "P"):
+                b = bank.setdefault(k, [None, [], []])
+                if b[0] != op["e"]:
+                    b[0], b[1], b[2] = op["e"], [], b[1]
+                e.update(b[2])
+                if op["e"] == "t":
+                    e.update(b[1])
+                b[1].append(n)
+            if grp is not None:
+                before[grp] = e
+            d.update(e)
+            for k in op["w"]:
+                lastw[k] = [n]
+                readers[k] = []
         if op["k"] != "r":
             for k in op["r"]:
                 readers.setdefault(k, []).append(n)
-        for k in op["w"]:
-            lastw[k] = n
-            readers[k] = []
         d.discard(n)
         deps.append(d)
     return deps
@@ -118,27 +116,37 @@ def _deps(ops):
 def _label(op):
     k = (op["w"] + op["r"] + ["-"])[0]
     if op["e"] == "t":
-        k += op["r"][1][:5]
-    return op["e"] + (k[0] + k[2:] if k[0] in "LTY" else k)
+        k += op["r"][1]
+    return op["e"] + (k[1:] if k[:2] == "Yf" else k[0] + k[2:] if k[0] in "LTXY" else k)
 
 
-def _order(ops, deps, seed):
+def _order(ops, deps):
     n = len(ops)
     succ = [[] for _ in range(n)]
     edges = [[(m, 0.0 if ops[m]["k"] == "w" or (ops[m]["e"] == "t" and ops[i]["e"] == "t") else ops[m]["lat"]) for m in deps[i]]
              + list(ops[i]["after"]) for i in range(n)]
+    named = {(o["rd"], _label(o)): i for i, o in enumerate(ops)}
+    for t in range(RO):
+        for e, names in ORDER:
+            row = [named[(t, e + x)] for x in names.split() if (t, e + x) in named]
+            for m, i in zip(row, row[1:]):
+                edges[i].append((m, 0.0))
     for i in range(n):
         for m, l in edges[i]:
             succ[m].append((i, l))
     pr = [0.0] * n
-    for i in range(n - 1, -1, -1):
+    left = [len(e) for e in edges]
+    topo_ = [i for i in range(n) if left[i] == 0]
+    for i in topo_:
+        for j, l in succ[i]:
+            left[j] -= 1
+            if left[j] == 0:
+                topo_.append(j)
+    assert len(topo_) == n
+    for i in reversed(topo_):
         pr[i] = ops[i]["d"] + max([l + pr[j] for j, l in succ[i]] + [0.0])
     for i in range(n):
-        pr[i] += PRIO.get(_label(ops[i]), 0)
-    x = seed
-    for i in range(n if seed else 0):
-        x = (x * 1103515245 + 12345) % 2147483648
-        pr[i] += CFG["jit"] * x / 2147483648.0
+        pr[i] += PRIO.get(_label(ops[i]), 0) + ops[i]["p"]
     left = [len(e) for e in edges]
     rdy = [0.0] * n
     free = {}
@@ -169,17 +177,17 @@ def _order(ops, deps, seed):
             left[j] -= 1
             if left[j] == 0:
                 ready.setdefault(ops[j]["e"], []).append(j)
-    return max(free.values()), order
+    return order, max(free.values())
 
 
 def _emit(g, T, ops):
     qs = {"v": g.vector, "s": g.scalar, "t": g.tensor, "g": g, "y": g.sync}
     deps = _deps(ops)
-    if not SEED:
-        SEED.append(min((_order(ops, deps, x)[0], x) for x in range(CFG["tries"]))[1])
-    order = _order(ops, deps, SEED[0])[1]
+    order = _order(ops, deps)[0]
     pos = {i: p for p, i in enumerate(order)}
-    seen, waits = {}, {}
+    seen, waits, members = {}, {}, {}
+    for i in order:
+        members.setdefault(ops[i].get("grp"), []).append(i)
     for i in order:
         op, best = ops[i], {}
         for m in deps[i]:
@@ -212,7 +220,10 @@ def _emit(g, T, ops):
             for s, v in op["sems"]:
                 q.wait_ge(T.sem[s], v)
             continue
-        ins = op["f"](q)
+        if op.get("grp") is None:
+            ins = op["f"](q)
+        else:
+            ins = op["f"](q, members[op["grp"]][0] == i, members[op["grp"]][-1] == i)
         if i in val:
             ins.then_inc(T.sem[val[i][0]], 16 if op["k"] == "d" else 1)
 
@@ -246,6 +257,8 @@ def rank_program(g, core, T, topo):
         _hand_on(g, core, T, topo)
         return
     C = CFG
+    NP = len(C["parts"])
+    cuts = C["cuts"]
     others = [c for c in T.cores if c != core]
     sib = [c for c in others if topo.chip(c) == topo.chip(core)][0]
     far = [c for c in others if topo.chip(c) != topo.chip(core)]
@@ -255,13 +268,15 @@ def rank_program(g, core, T, topo):
     e_near = [e for e in e_all if e not in e_far]
     hf = len(e_far) // 2
     plan3 = [(far[0], e_far[:hf]), (far[1], e_far[hf:]), (sib, e_near)]
-    prank, srank = T.rank_of(peer), T.rank_of(sib)
+    srank = T.rank_of(sib)
     franks = [T.rank_of(c) for c in far]
     ops = []
+    low = [0.0]
+    rd = [-1]
 
     def op(e, f, r, w, d, k="c", lat=None, after=(), **kw):
         o = {"e": e, "f": f, "r": list(r), "w": list(w), "k": k, "d": d, "lat": C["hop"] if lat is None else lat,
-             "after": list(after)}
+             "after": list(after), "p": low[0], "rd": rd[0]}
         o.update(kw)
         ops.append(o)
         return len(ops) - 1
@@ -270,7 +285,7 @@ def rank_program(g, core, T, topo):
         return op(e, None, r, w, 0.0, k="w", sems=sems, after=after)
 
     def dur(n, gth=False):
-        return 50.0 + n * C["gam"] * C["cyc"] if gth else max(64.0, n) * C["cyc"] + C["ovh"]
+        return 55.0 + n * C["gam"] * C["cyc"] if gth else max(64.0, n) * C["cyc"] + C["ovh"]
 
     def ts(out, in0, s1, s2, o0, o1, r, w, n, gth=False):
         if s2 is None:
@@ -284,8 +299,21 @@ def rank_program(g, core, T, topo):
     def act(out, in_, fn, bias, scale, r, w, n, gth=False):
         op("s", lambda q: q.activation(out, in_, fn, bias=bias, scale=scale), r, w, dur(n, gth))
 
+    def shift(e, out, in_, c, r, w, n):
+        if e == "s":
+            act(out, in_, F.Identity, c, 1.0, r, w, n)
+        else:
+            ts(out, in_, c, None, A.add, None, r, w, n)
+
+    def fill(out, c, w):
+        op("v", lambda q: q.memset(out, c), [], w, 83.0)
+
     def mm(out, lhsT, rhs, start, stop, r, w, n, f32=False):
         op("t", lambda q: q.matmul(out, lhsT, rhs, start, stop), r, w, max(64, n) * (4 if f32 else 1) * C["pe"] + C["pov"], lat=C["hop"] + 45)
+
+    def acc(grp, out, lhsT, rhs, r, w, n):
+        op("t", lambda q, start, stop: q.matmul(out, lhsT, rhs, start, stop), r, w, max(64, n) * C["pe"] + C["pov"],
+           lat=C["hop"] + 45, grp=grp + str(rd[0]))
 
     def iota(out, pat, base, cm, w, n, flt=True):
         if flt:
@@ -306,16 +334,25 @@ def rank_program(g, core, T, topo):
                    after=[(gq[0], gap)] if gq[0] is not None else [])
         return gq[0]
 
+    ps, b0 = [], 0
+    for n in C["parts"]:
+        ps.append((b0, n))
+        b0 += n
+
     for j in range(4):
         op("ys"[j % 2], lambda q, j=j: q.dma_start(T.Z[:, 256 * j:256 * j + 256], T.kin[:, 256 * j:256 * j + 256]),
-           [], ["Z%d" % j], 50.0, k="d", sem="ld%d" % j, lat=2500.0 + 400 * j)
+           [], ["Z%d" % j], 50.0, k="d", sem="ld%d" % j, lat=2200.0 + 300 * j)
     iota(T.ci[:, 0:1], [[0, 1]], 0, 1, ["ci0"], 1, flt=False)
-    iota(T.xc[:], [[1, 144]], 0, 0, ["xc"], 144)
+    iota(T.xc[:], [[1, 256]], 0, 0, ["xc"], 256)
     iota(T.pw[:], [[0, 128]], 0, 1, ["pw"], 128)
     iota(T.xg[:], [[16, 8], [0, 16]], 0, 0, ["xg"], 128)
-    op("v", lambda q: q.memset(T.Vw[:], 0.0), [], ["Vw"], 64.0)
-    op("v", lambda q: q.memset(T.Vm[:], -1.0), [], ["Vm"], 64.0)
-    op("v", lambda q: q.memset(T.Vw[:, 3:4], 2.0), [], ["Vw"], 64.0)
+    fill(T.Vw[:], 0.0, ["Vw"])
+    fill(T.Vw[:, 3:4], 2.0, ["Vw"])
+    fill(T.Vm[:], 0.0, ["Vm"])
+    fill(T.Vm[:, 0:4], -1.0, ["Vm"])
+    fill(T.vr[:], 0.0, ["vr"])
+    fill(T.vr[:, 4:5], 1.0, ["vr"])
+    fill(T.vr[:, 5:6], -1.0, ["vr"])
 
     def ci(j):
         return T.ci[:, j:j + 1]
@@ -330,79 +367,82 @@ def rank_program(g, core, T, topo):
     ts(cf(2), ci(1), 0.0, None, A.add, None, ["ci1"], ["cf2"], 1)
     ts(cf(3), ci(2), 62.5, cf(0), A.mult, A.add, ["ci2", "cf0"], ["cf3"], 1)
     ts(cf(4), ci(2), -62.5, cf(0), A.mult, A.add, ["ci2", "cf0"], ["cf4"], 1)
-    ts(cf(5), ci(3), -LN2, -LN2 * 330.0, A.mult, A.add, ["ci3"], ["cf5"], 1)
+    ts(cf(5), ci(3), -LN2, -LN2 * 1354.0, A.mult, A.add, ["ci3"], ["cf5"], 1)
     ts(cf(6), ci(5), 1.5, 1.0, A.mult, A.add, ["ci5"], ["cf6"], 1)
     ts(cf(7), ci(4), 1.0, cf(6), A.add, A.mult, ["ci4", "cf6"], ["cf7"], 1)
-    ts(cf(8), cf(7), 0.0625, None, A.mult, None, ["cf7"], ["cf8"], 1)
+    act(cf(9), cf(0), F.Sigmoid, -3.5 * 256.0, 256.0, ["cf0"], ["cf9"], 1)
+    ts(cf(10), cf(9), -1.0, 1.0, A.mult, A.add, ["cf9"], ["cf10"], 1)
+    ts(cf(11), cf(9), 192.0, None, A.mult, None, ["cf9"], ["cf11"], 1)
+    ts(cf(12), cf(7), cf(10), cf(11), A.mult, A.add, ["cf7", "cf10", "cf11"], ["cf12"], 1)
+    ts(cf(8), cf(12), 0.0625, None, A.mult, None, ["cf12"], ["cf8"], 1)
+    ts(cf(13), cf(9), 1008.0, 16.0, A.mult, A.add, ["cf9"], ["cf13"], 1)
+    ts(cf(15), cf(9), 1024.0, None, A.mult, None, ["cf9"], ["cf15"], 1)
+    ts(cf(14), ci(4), 2.0, -1.0, A.mult, A.add, ["ci4"], ["cf14"], 1)
+    ts(cf(14), cf(14), cf(9), None, A.mult, None, ["cf14", "cf9"], ["cf14"], 1)
+    for s in range(4):
+        ts(cf(16 + s), cf(14), 256.0 * (16.0 * (1024 * rank + s) - MID), -128.0, A.mult, A.add, ["cf14"], ["cw%d" % s], 1)
     x128 = T.xc[:, 0:128]
     for c in range(2):
         for gm in range(2):
             sh = -16.0 * gm if c == 0 else -16.0 * (gm - 1) - 1000.0
             j = 2 * c + gm
             ts(T.Pm[:, 128 * j:128 * j + 128], x128, sh, cf(3 + c), A.add, A.is_equal, ["xc", "cf3", "cf4"], ["cPm%d" % j], 128)
-    eye = [("If", 1.0), ("Ih", -16.0), ("I8k", 8192.0), ("I16", 16.0), ("I256", 256.0), ("Isk", -1024.0),
-           ("I16f", 16.0), ("Im15", -15.0)]
-    if C["prep"]:
-        eye.append(("Imf", -1.0))
-    eye.append(("Im32", -32.0))
-    for nm, wgt in eye:
+    for nm, wgt in (("Imf", -1.0), ("Im15", -15.0), ("Im16", -16.0), ("Im1h", -1.0)):
         ts(T[nm][:], x128, cf(0), wgt, A.is_equal, A.mult, ["xc", "cf0"], [nm], 128)
-    ts(T.R64[:], T.xc[:], cf(1), 64.0, A.is_equal, A.mult, ["xc", "cf1"], ["R64"], 144)
-    if any(C["kc"]):
-        ts(T.R16[:], T.xc[:], cf(1), 16.0, A.is_equal, A.mult, ["xc", "cf1"], ["R16"], 144)
-    ts(T.c1[:], x128, cf(0), -2.0, A.is_equal, A.mult, ["xc", "cf0"], ["c1"], 128)
+    for nm, wgt, c in (("I8k", 8192.0, 0.0), ("I16", 16.0, 0.0), ("I256", 256.0, 0.0), ("I16f", 16.0, 0.0), ("Im32", -32.0, 0.0),
+                       ("I1", 1.0, 0.0), ("Im1", -1.0, 0.0), ("Ims", -0.0625, 0.0), ("Ob", 49152.0, 512.0),
+                       ("Om", 0.0, -256.0), ("O1", 0.0, 1.0)):
+        act(T[nm][:], T.Imf[:], F.Identity, c, -wgt, ["Imf"], [nm], 128)
+    ts(T.R64[:], T.xc[:, 0:144], cf(1), 64.0, A.is_equal, A.mult, ["xc", "cf1"], ["R64"], 144)
+    act(T.R16[:], T.R64[:], F.Identity, 0.0, 0.25, ["R64"], ["R16"], 144)
     ts(T.c2[:], T.xg[:], cf(2), None, A.is_equal, None, ["xg", "cf2"], ["c2"], 128)
-    tt(T.Ym[:], T.c1[:], T.c2[:], A.add, ["c1", "c2"], ["Ym"], 256)
-    op("v", lambda q: q.memset(T.Om[:], -256.0), [], ["Om"], 64.0)
-    op("v", lambda q: q.memset(T.O16[:], 16.0), [], ["O16"], 64.0)
-    ts(T.c1[:], x128, cf(0), 49152.0, A.is_equal, A.mult, ["xc", "cf0"], ["c1"], 128)
-    ts(T.Ob[:], T.c1[:], 512.0, None, A.add, None, ["c1"], ["Ob"], 128)
-    ts(T.Nw[:, 0:128], T.pw[:], 0.0, cf(8), A.mult, A.add, ["pw", "cf8"], ["Nw0"], 128)
-    ts(T.Nw[:, 128:256], T.pw[:], 0.0, cf(7), A.mult, A.add, ["pw", "cf7"], ["Nw1"], 128)
+    op("g", lambda q: q.affine_select(T.Ym[:], T.c2[:], [[-1, 128]], A.not_equal, -1.0, 0, 1), ["c2"], ["Ym"], 400.0)
+    for o, j, k in ((T.Nw[:, 0:128], 8, "Nw0"), (T.Nw[:, 128:256], 12, "Nw1"), (T.O16[:], 13, "O16"), (T.Osk[:], 15, "Osk")):
+        act(o, T.pw[:], F.Identity, cf(j), 0.0, ["pw", "cf%d" % j], [k], 128)
+    for j in range(4):
+        ts(T.Bw[:, 128 * j:128 * j + 128], T.pw[:], float(j), -1.0, A.is_equal, A.mult, ["pw"], ["Bw%d" % j], 128)
+    act(T.Iv[:], T.vr[:], F.Identity, 0.0, -64.0, ["vr"], ["Iv"], 8)
+    act(T.xi[:], T.xc[:], F.Identity, 0.0, 1.0, ["xc"], ["xi"], 256)
+    for ch, (b, n) in enumerate(ps):
+        for j in range(4):
+            act(T.Cr[0:32, 4 * b + n * j:4 * b + n * j + n], T.xc[0:32, 0:n], F.Identity,
+                32.0 + 2 ** j + (1536.0 if j == 3 else -192.0 * 2 ** j), 0.0, ["xc"], ["Cr%d%d" % (ch, j)], n)
 
     PDk = [(T.PD0, "PD0"), (T.PD1, "PD1")]
     OWN = ["To%d" % j for j in range(4)]
-    snd = []
     for j in range(4):
         pb, pk = PDk[j % 2]
+        low[0] = 1000.0 * (4 - j)
         zs, cs = T.Z[:, 256 * j:256 * j + 256], T.Tb[:, 1024 * rank + 256 * j:1024 * rank + 256 * j + 256]
         i1 = T.i1[:, 256 * j:256 * j + 256]
         ts(i1, zs, 15, None, A.bitwise_and, None, ["Z%d" % j], ["i1%d" % j], 256)
         ts(pb[:, 0:256], i1, -0.9375, None, A.mult, None, ["i1%d" % j], [pk + "a"], 256)
         tt(cs, zs, pb[:, 0:256], A.add, ["Z%d" % j, pk + "a"], [OWN[j]], 256)
-        snd.append(send([(_helper(T, topo, core), e_far), (sib, e_near)], cs, ["fw%d" % j, "arI"], "lsI", [OWN[j]]))
+        send([(_helper(T, topo, core), e_far), (sib, e_near)], cs, ["fw%d" % j, "arI"], "lsI", [OWN[j]])
+    low[0] = 0.0
     for e in "vs":
         wait(e, [("arI", 4 * (len(e_near) + len(e_all))), ("lsI", 4 * len(e_all))], ["in" + e], after=[(gq[0], 9000.0)])
 
     PA = [(T.PA0, "PA0"), (T.PA1, "PA1")]
     PW = [(T.PW0, "PW0"), (T.PW1, "PW1")]
 
-    def parts(t):
-        ps, b = [], 0
-        for n, off, step in C["parts"]:
-            if t == RO - 1:
-                off, step = b, 1
-            ps.append((b, n, off, step))
-            b += n
-        return ps
-
     def tkeys(s):
-        return OWN + ["T%d" % s]
+        return OWN + ["T%d_%d" % (s, rank), "X%d_%d" % (s, rank)]
 
-    def cols(buf, r, s, p):
-        b, n, off, step = p
-        c0 = 1024 * r + 4 * off + s
-        return buf[:, c0:c0 + 4 * step * (n - 1) + 1:4 * step]
+    def cols(buf, r, s, b, n):
+        c0 = 1024 * r + 4 * b + s
+        return buf[:, c0:c0 + 4 * (n - 1) + 1:4]
 
     def prep(t):
         s = t % 4
         tk = tkeys(s)
-        for ch, p in enumerate(parts(t)):
-            b, n = p[0], p[1]
-            h = slice(b, b + n)
-            u = cols(T.Tb, rank, s, p)
-            ts(T.ph[:, h], u, 0.0625, -2048.0, A.mult, A.add, tk, ["ph%d" % ch], n)
-            op("v", lambda q, h=h: q.transpose(T.pt[:, h], T.ph[:, h]), ["ph%d" % ch], ["pt%d" % ch], dur(n / 2))
+        u = cols(T.Tb, rank, s, 0, 256)
+        ts(T.Sel[:, 128 * t:128 * t + 128], T.pw[:], float(17 * t + 3), None, A.is_equal, None, ["pw"], ["Sel", "Sel%d" % t], 128)
+        ts(cf(20 + t), cf(0), float(17 * t + 3), None, A.is_equal, None, ["cf0"], ["cs", "cs%d" % t], 1)
+        ts(T.Sv[:, 8 * t:8 * t + 8], T.vr[:], cf(20 + t), None, A.mult, None, ["vr", "cs%d" % t], ["Sv", "Sv%d" % t], 8)
+        ts(T.ph[:], u, 0.0625, -2048.0, A.mult, A.add, tk, ["ph"], 256)
+        op("v", lambda q: q.transpose(T.pt[:], T.ph[:]), ["ph"], ["pt"], dur(128))
+        for ch, (b, n) in enumerate(ps):
             nh = n // 16
             for bb in range(n // 32):
                 for c in range(2):
@@ -411,83 +451,62 @@ def rank_program(g, core, T, topo):
                         j = 2 * c + gm
                         x = b + 32 * bb + 16 * gm
                         mm(T.PX[:, o:o + 15 * nh + 1:nh], T.Pm[:, 128 * j:128 * j + 128], T.pt[:, x:x + 16], gm == 0, gm == 1,
-                           ["cPm%d" % j, "pt%d" % ch], ["PX_o"], 16)
+                           ["cPm%d" % j, "pt"], ["PX_o"], 16)
         ts(T.Of[:], T.PX[:, 0:256], 2048.0, None, A.add, None, ["PX_o"], ["Of"], 256)
-        for ch, p in enumerate(parts(t)):
-            b, n, off, step = p
-            h = slice(b, b + n)
-            u = cols(T.Tb, rank, s, p)
-            ts(T.zi[:, h], u, -16.0, 1048575.0, A.mult, A.add, tk, ["zi%d" % ch], n)
-            ts(T.nm[:, h], u, BIG, -BIG, A.add, A.add, tk, ["nm%d" % ch], n)
+        ts(T.nm[:], u, BIG, -BIG - MID, A.add, A.add, tk, ["nm"], 256)
+        mm(T.PD0[:, 0:256], T.I16f[:], u, True, False, tk + ["I16f"], ["PD0a"], 256, True)
+        mm(T.PD0[:, 0:256], T.Im16[:], T.nm[:], False, True, ["nm", "Im16"], ["PD0a"], 256)
+        for ch, (b, n) in enumerate(ps):
             pa, pk = PA[(4 * b) // 512]
+            x = 4 * b % 512
+            hk = ["H%d%d" % (ch, j) for j in range(4)]
+            ak = [pk + "%d%d" % (ch, j) for j in range(4)]
             for j in range(4):
-                x = 4 * b + n * j
-                ts(T.Aq[:, x:x + n], T.zi[:, h], 32 + (1 << j), None, A.bitwise_and, None, ["zi%d" % ch], ["Aq%d%d" % (ch, j)], n)
-            op("v", lambda q, o=pa[:, 4 * b % 512:4 * b % 512 + 4 * n], i=T.Aq[:, 4 * b:4 * b + 4 * n]: q.tensor_copy(o, i),
-               ["Aq%d%d" % (ch, j) for j in range(4)], [pk + "%d%d" % (ch, j) for j in range(4)]
-               + (["PA0%s%d" % (u, v) for u in "nt" for v in range(NP)] if ch == 0 else []), dur(4 * n))
-            iota(T.at[:, h], [[64 * step, n]], 16 * (1024 * rank + 4 * off + s), 0, ["at%d" % ch], n)
-        x = 128 * (t % 2)
-        ts(T.Sel[:, x:x + 128], T.pw[:], float(17 * t + 3), None, A.is_equal, None, ["pw"], ["Sel%d" % (t % 2)], 128)
+                act(T.H[:, 4 * b + n * j:4 * b + n * j + n], T.PD0[:, b:b + n], F.Identity,
+                    192.0 * 2 ** j - (2 ** j - 1) / 2.0 - 16.0 * MID, 1.0, ["PD0a"], [hk[j]], n)
+            mm(pa[:, x:x + 4 * n], T.O1[0:1, :], T.Cr[0:1, 4 * b:4 * b + 4 * n], True, False,
+               ["O1"] + ["Cr%d%d" % (ch, j) for j in range(4)], ak, 4 * n)
+            mm(pa[:, x:x + 3 * n], T.I1[:], T.H[:, 4 * b + n:4 * b + 4 * n], False, False, ["I1"] + hk, ak, 3 * n)
+            mm(pa[:, x:x + 4 * n], T.Im1[:], T.H[:, 4 * b:4 * b + 4 * n], False, True, ["Im1"] + hk, ak, 4 * n)
 
     def decode(s):
         tk = tkeys(s)
-        u = T.Tb[:, 1024 * rank + s:1024 * rank + 1024:4]
-        act(T.du[:], u, F.Identity, BIG, 1.0, tk, ["du"], 256)
-        act(T.dn[:], T.du[:], F.Identity, -BIG, 1.0, ["du"], ["dn"], 256)
-        mm(T.PD0[:, 0:256], T.I16f[:], u, True, False, tk + ["I16f"], ["PD0a"], 256, True)
-        mm(T.PD0[:, 0:256], T.Im15[:], T.dn[:], False, True, ["dn", "Im15"], ["PD0a"], 256, True)
-        act(T.Yo[:, s:1024:4], T.PD0[:, 0:256], F.Identity, 0.0, 1.0, ["PD0a"], ["Y%d" % s], 256)
+        u = cols(T.Tb, rank, s, 0, 256)
+        ts(T.dn[:], u, BIG, -BIG - MID, A.add, A.add, tk, ["dn"], 256)
+        mm(T.PD1[:, 0:256], T.I16f[:], u, True, False, tk + ["I16f"], ["PD1a"], 256, True)
+        mm(T.PD1[:, 0:256], T.Im15[:], T.dn[:], False, True, ["dn", "Im15"], ["PD1a"], 256)
+        act(T.Yo[:, s:1024:4], T.PD1[:, 0:256], F.Identity, -15.0 * MID, 1.0, ["PD1a"], ["Y%d" % s], 256)
 
     prep(0)
     win_all = T.Tb[:, 0:4096]
-    TALL = OWN + ["T%d" % s for s in range(4)]
+    TALL = OWN + [k + "%d_%d" % (s, r) for k in "TX" for s in range(4) for r in range(4)]
     pdn = [0]
     nsent = 0
 
     for t in range(RO):
         s = t % 4
         last = t == RO - 1
-        ps = parts(t)
-        sel, selk = T.Sel[:, 128 * (t % 2):128 * (t % 2) + 128], "Sel%d" % (t % 2)
+        sel, selk = T.Sel[:, 128 * t:128 * t + 128], "Sel%d" % t
         sends = []
+        rd[0] = t
 
-        def bcast(ch):
-            b, n = ps[ch][0], ps[ch][1]
-            bp, bk = (T.PX[:, 384:384 + n], "PX_b") if ch == 0 else (T.PM[:, 256 + b:256 + b + n], "PM_b%d" % ch)
-            if C["wide"]:
-                bp, bk = T.PX[:, 256 + b:256 + b + n], "PX_b%d" % ch
-            nh = n // 16
-            ts(T.Gb[:, b:b + n], win_all.indirect(T.Of[:, b + nh * t:b + nh * (t + 1)]), BIG, -BIG, A.add, A.add,
-               TALL + ["Of", "inv"], ["Gb%d" % ch], n, True)
-            mm(bp, sel, T.Gb[:, b:b + n], True, True, [selk, "Gb%d" % ch], [bk], n, True)
-            return bp, bk
-
-        def head(ch, bp, bk):
-            b, n, off, step = ps[ch]
+        def head(ch):
+            b, n = ps[ch]
             h = slice(b, b + n)
             c = str(ch)
-            for u in range(C["vw"][ch] // n):
-                o = T.Bv[:, 512 * ch + n * u:512 * ch + n * u + n]
-                if C["evs"] and ch > 0:
-                    act(o, bp, F.Identity, -OFF, 1.0, [bk], ["Bv%s%d" % (c, u)], n)
-                else:
-                    ts(o, bp, -OFF, None, A.add, None, [bk], ["Bv%s%d" % (c, u)], n)
-            if C["wide"]:
-                if ch == 0:
-                    bp, al = T.PX[:, 256:512], [str(x) for x in range(NP)]
-                    bk = ["PX_b" + x for x in al]
-                    ts(T.Bh[:], bp, 0.0625, -2048.0, A.mult, A.add, bk, ["Bh" + x for x in al], 256)
-                    tt(T.own[:], T.nm[:], bp, A.is_equal, ["nm" + x for x in al] + bk, ["own" + x for x in al], 256)
-                    tt(T.skp[:], T.at[:], bp, A.is_equal, ["at" + x for x in al] + bk, ["skp" + x for x in al], 256)
-                return
-            if C["ks"][ch]:
-                ts(T.Bh[:, h], bp, 0.0625, -2048.0, A.mult, A.add, [bk], ["Bh" + c], n)
-            tt(T.own[:, h], T.nm[:, h], bp, A.is_equal, ["nm" + c, bk], ["own" + c], n)
-            tt(T.skp[:, h], T.at[:, h], bp, A.is_equal, ["at" + c, bk], ["skp" + c], n)
+            nh = n // 16
+            vw = C["vw"][ch]
+            bp, bk = [(T.PX, "PX_b0"), (T.PM, "PM_b1"), (T.PX, "PX_b2")][ch]
+            x = 256 if ch == 2 else 0
+            ts(T.Gb[:, h], win_all.indirect(T.Of[:, b + nh * t:b + nh * (t + 1)]), BIG, -BIG - MID, A.add, A.add,
+               TALL + ["Of", "inv"], ["Gb" + c], n, True)
+            for u in range(vw // n):
+                mm(bp[:, x + n * u:x + n * u + n], sel, T.Gb[:, h], True, True, [selk, "Gb" + c], [bk], n)
+            shift(C["bvs"][ch], T.Bv[:, 512 * ch:512 * ch + vw], bp[:, x:x + vw], MID - OFF, [bk], ["Bv" + c], vw)
+            tt(T.own[:, h], T.nm[:, h], bp[:, x:x + n], A.is_equal, ["nm", bk], ["own" + c], n)
 
         def body(ch):
-            b, n, off, step = ps[ch]
+            b, n = ps[ch]
             h = slice(b, b + n)
             nh = n // 16
             c = str(ch)
@@ -502,28 +521,26 @@ def rank_program(g, core, T, topo):
                 return slice(16 * b + n * k, 16 * b + n * (k + m))
 
             red = []
-            gs = 512 // n
             k = 16 - nks
             while k < 16:
-                m = min(gs, 16 - k, (nks + 1) // 2 if nks > gs else gs)
+                m = min(C["sw"][ch] // n, 16 - k)
                 pb, pk = PDk[pdn[0] % 2]
                 pdn[0] += 1
                 act(T.G[:, sl(k, m)], gath(k, m), F.Identity, 0.0, 1.0, TALL + ["Of", "ins"], ["G%s_%d" % (c, k)], n * m, True)
-                mm(pb[:, 0:n * m], T.If[:], T.G[:, sl(k, m)], True, False, ["If", "G%s_%d" % (c, k)], [pk + "a"], n * m, True)
+                mm(pb[:, 0:n * m], T.Imf[:], T.G[:, sl(k, m)], True, False, ["Imf", "G%s_%d" % (c, k)], [pk + "a"], n * m, True)
                 for u in range(m):
-                    mm(pb[:, n * u:n * u + n], T.Ih[:], T.Bh[:, h], False, u == m - 1, ["Ih", "Bh" + c], [pk + "a"], n)
-                act(T.Cl[:, sl(k, m)], pb[:, 0:n * m], F.Sigmoid, -32768.0 + OFF - 2.0, 1.0, [pk + "a"],
+                    mm(pb[:, n * u:n * u + n], sel, T.Gb[:, h], False, u == m - 1, [selk, "Gb" + c], [pk + "a"], n)
+                act(T.Cl[:, sl(k, m)], pb[:, 0:n * m], F.Sigmoid, OFF - 2.0 - MID, -1.0, [pk + "a"],
                     ["Cl%s_%d" % (c, k + u) for u in range(m)], n * m)
                 red.append([(k + u, "R64") for u in range(m)])
                 k += m
             vred = []
-            f = C["first"][ch]
-            ks = ([0] if f else []) + list(range(f, 16 - nks, kk))
+            ks = list(range(0, 16 - nks, kk))
             for x, k in enumerate(ks):
                 m = (ks + [16 - nks])[x + 1] - k
                 dk = "Dv%s_%d" % (c, k)
                 tt(T.Dv[:, sl(k, m)], gath(k, m), T.Bv[:, 512 * ch:512 * ch + n * m], A.subtract,
-                   TALL + ["Of", "inv"] + ["Bv%s%d" % (c, u) for u in range(m)], [dk], n * m, True)
+                   TALL + ["Of", "inv", "Bv" + c], [dk], n * m, True)
                 w = ["Cl%s_%d" % (c, k + u) for u in range(m)]
                 mine = x >= len(ks) - C["kc"][ch]
                 if mine:
@@ -531,47 +548,52 @@ def rank_program(g, core, T, topo):
                 else:
                     act(T.Cl[:, sl(k, m)], T.Dv[:, sl(k, m)], F.Sigmoid, -2.0, 1.0, [dk], w, n * m)
                 vred.append([(k + u, "R16" if mine else "R64") for u in range(m)])
-            seq = []
-            for x in range(len(vred)):
-                seq += vred[x]
-                if x >= 1 and red:
-                    seq += red.pop(0)
-            for x in red:
-                seq += x
-            for x, (k, R) in enumerate(seq):
-                if x == len(seq) - 2:
-                    mm(pw_[:, 0:n], T.I8k[:], T.own[:, h], False, False, ["I8k", "own" + c], [wk + "w"], n)
-                mm(pw_[:, 0:n], T[R][:, 15 - k:143 - k], T.Cl[:, sl(k)], x == 0, x == len(seq) - 1,
-                   [R, "Cl%s_%d" % (c, k)], [wk + "w"], n)
+            acc("w" + c, pw_[:, 0:n], T.I8k[:], T.own[:, h], ["I8k", "own" + c], [wk + "w"], n)
+            for k, R in sum(red + vred, []):
+                acc("w" + c, pw_[:, 0:n], T[R][:, 15 - k:143 - k], T.Cl[:, sl(k)], [R, "Cl%s_%d" % (c, k)], [wk + "w"], n)
 
-        def oldof(ch):
-            if last:
-                return cols(T.Yo, 0, s, ps[ch]), ["Y%d" % s]
-            return cols(T.Tb, rank, s, ps[ch]), tkeys(s)
-
-        def land(gr, r0, r1):
-            x = 1024 * t + 512 * gr
-            return T.L[:, x + 128 * r0:x + 128 * r1]
+        def land(r, b, n):
+            x = 1024 * t + 256 * r + b
+            return T.L[:, x:x + n]
 
         def tail(ch):
-            b, n, off, step = ps[ch]
+            b, n = ps[ch]
             h = slice(b, b + n)
             c = str(ch)
             pw_, wk = PW[ch % 2]
             pa, pk = PA[(4 * b) // 512]
-            old, ok = oldof(ch)
+            old, ok = (cols(T.Yo, 0, s, b, n), ["Y%d" % s]) if last else (cols(T.Tb, rank, s, b, n), tkeys(s))
 
             def pl(buf, j, m=1):
                 return buf[:, 4 * b + n * j:4 * b + n * (j + m)]
 
             ts(T.W[:, h], pw_[:, 0:n], 7.5, 2080.0, A.add, A.min, [wk + "w"], ["W" + c], n)
+            dl, dk, td, tk = pw_[:, 128:128 + n], wk + "n", pw_[:, 384:384 + n], wk + "t"
+            free = ch == NP - 1 or (4 * ps[ch + 1][0]) // 512 != (4 * b) // 512
+            ey, ek = (pa, pk + "e") if free else (T.PM, "PM_e")
+            if ch == NP - 1:
+                ey, ek = T.PX, "PX_e"
+            if ch + 2 < NP:
+                dl, dk, td, tk = pa[:, 0:n], pk + "n", pa[:, 384:384 + n], pk + "t"
+                ey, ek = T.PM, "PM_e"
+
+            def delta():
+                acc("d" + c, dl, sel, T.Gb[:, h], [selk, "Gb" + c], [dk], n)
+                acc("d" + c, dl, T.Im1h[:], T.nm[:, h], ["Im1h", "nm"], [dk], n)
+                acc("d" + c, dl, T["Im1" if last else "Ims"][:], pl(T.H, 0), ["Ims", "H%s0" % c, "Im1"], [dk], n)
+
+            if ch + 2 >= NP:
+                delta()
             for j in range(4):
                 ts(pl(T.Q, j), T.W[:, h], 32 + (1 << j), None, A.bitwise_and, None, ["W" + c], ["Q%s%d" % (c, j)], n)
             ts(T.tes[:, h], pl(T.Q, 0), 32.0, None, A.is_ge, None, ["Q%s0" % c], ["tes" + c], n)
-            vb, vk = (T.PD0, "PD0a") if ch == NP - 1 else (T.PM, "PM_v")
-            mm(vb[0:4, 0:n], T.Vm[:, 0:4], T.tes[:, h], True, False, ["Vm", "tes" + c], [vk], n)
-            split = C["split"] and ch == NP - 1
-            xb = [(T.PX, "PX_x", 0), (T.PD1, "PD1a", 0) if split else (T.PX, "PX_x", 2 * n)]
+            vb, vk = T.PM[0:6, 0:n], "PM_v"
+            acc("v" + c, vb, T.Sv[:, 8 * t:8 * t + 6], T.Gb[:, h], ["Sv%d" % t, "Gb" + c], [vk], n)
+            acc("v" + c, vb, T.Iv[0:1, 0:6], T.xi[0:1, h], ["Iv", "xi"], [vk], n)
+            acc("v" + c, vb, T.Vm[:, 0:6], T.tes[:, h], ["Vm", "tes" + c], [vk], n)
+            split = len(C["fds"][ch]) == 2
+            xs = C["xs"][ch]
+            xb = [(T.PD0, "PD0a", 0), (T.PD1, "PD1a", 0)] if split else [(T.PX, "PX_x", 0), (T.PX, "PX_x", 2 * n)]
             for u in range(2):
                 x = (4 * b + 2 * n * u) % 512
                 if not C["e1"][ch]:
@@ -584,41 +606,45 @@ def rank_program(g, core, T, topo):
                        ["E%s0" % c, "E%s1" % c], 4 * n)
                 for j in range(2):
                     o = xb[u][0][:, xb[u][2] + n * j:xb[u][2] + n * j + n]
-                    mm(o, T.Om[:], T.tes[:, h], True, False, ["Om", "tes" + c], [xb[u][1]], n)
-                    mm(o, T.Ob[:], pl(T.E, 2 * u + j), False, True, ["Ob", "E%s%d" % (c, u)], [xb[u][1]], n)
-            if NP == 2:
-                dl, dk, td, tk = pw_[:, 128:128 + n], wk + "n", pw_[:, 384:384 + n], wk + "t"
-            else:
-                dl, dk, td, tk = T.PA0[:, b:b + n], "PA0n" + c, T.PA0[:, 256 + b:256 + b + n], "PA0t" + c
+                    if not xs:
+                        mm(o, T.Om[:], T.tes[:, h], True, False, ["Om", "tes" + c], [xb[u][1]], n)
+                        mm(o, T.Ob[:], pl(T.E, 2 * u + j), False, True, ["Ob", "E%s%d" % (c, u)], [xb[u][1]], n)
             for j in range(4):
-                mm(vb[0:4, 0:n], T.Vw[:, 3 - j:7 - j], pl(T.E, j), False, j == 3, ["Vw", "E%s%d" % (c, j // 2)], [vk], n)
-            act(T.won[0:4, h], vb[0:4, 0:n], F.Sigmoid, -128.0, 256.0, [vk], ["won" + c], n)
-            mm(dl, sel, T.Gb[:, h], True, False, [selk, "Gb" + c], [dk], n, True)
-            mm(dl, T.Imf[:], old, False, False, ["Imf"] + ok, [dk], n, True)
-            if split:
-                act(pl(T.Fd, 0, 2), T.PX[:, 0:2 * n], F.Sigmoid, -49280.0, 1.0, ["PX_x"], ["Fd%s0" % c], 2 * n)
-                ts(pl(T.Fd, 2, 2), T.PD1[:, 0:2 * n], 49280.0, None, A.is_gt, None, ["PD1a"], ["Fd%s1" % c], 2 * n)
-            elif C["t4s"]:
-                act(pl(T.Fd, 0, 4), T.PX[:, 0:4 * n], F.Sigmoid, -49280.0, 1.0, ["PX_x"], ["Fd%s0" % c, "Fd%s1" % c], 4 * n)
-            else:
-                ts(pl(T.Fd, 0, 4), T.PX[:, 0:4 * n], 49280.0, None, A.is_gt, None, ["PX_x"], ["Fd%s0" % c, "Fd%s1" % c], 4 * n)
-            e = T.PM[:, 128:128 + n]
-            mm(e, T.I256[:], T.tes[:, h], True, False, ["I256", "tes" + c], ["PM_e"], n)
-            mm(e, T.I256[:], T.own[:, h], False, False, ["I256", "own" + c], ["PM_e"], n)
-            mm(e, T.Isk[:], T.skp[:, h], False, False, ["Isk", "skp" + c], ["PM_e"], n)
+                acc("v" + c, vb, T.Vw[:, 3 - j:9 - j], pl(T.E, j), ["Vw", "E%s%d" % (c, j // 2)], [vk], n)
+            act(T.won[0:6, h], vb, F.Sigmoid, T.cf[0:6, 16 + s:17 + s], 256.0, [vk, "cw%d" % s], ["won" + c], n)
+            for u in range((2 if split else 1) if xs else 0):
+                m = 2 if split else 4
+                mm(xb[u][0][:, 0:m * n], T.I1[:], pl(T.E, m * u, m), True, False,
+                   ["I1"] + ["E%s%d" % (c, x) for x in ([u] if split else [0, 1])], [xb[u][1]], m * n)
+                for j in range(m):
+                    mm(xb[u][0][:, n * j:n * j + n], T.Bw[0:4, 128 * (m * u + j):128 * (m * u + j + 1)], T.won[0:4, h], False, j == m - 1,
+                       ["Bw%d" % (m * u + j), "won" + c], [xb[u][1]], n)
+            for u, e in enumerate(C["fds"][ch]):
+                m = 2 if split else 4
+                o, i, r, w = pl(T.Fd, m * u, m), xb[u][0][:, 0:m * n], [xb[u][1]], ["Fd%s%d" % (c, x) for x in ([u] if split else [0, 1])]
+                if e == "s":
+                    act(o, i, F.Abs if xs else F.Sigmoid, 0.0 if xs else -49280.0, 1.0, r, w, m * n)
+                else:
+                    ts(o, i, 0.0 if xs else 49280.0, None, A.not_equal if xs else A.is_gt, None, r, w, m * n)
+            if ch + 2 < NP:
+                delta()
+            e = ey[:, 128:128 + n]
+            acc("e" + c, e, T.I256[:], T.tes[:, h], ["I256", "tes" + c], [ek], n)
+            acc("e" + c, e, T.I256[:], T.own[:, h], ["I256", "own" + c], [ek], n)
+            for j in range(0 if xs else 4):
+                acc("e" + c, e, T.I16[:], pl(T.E, j), ["I16", "E%s%d" % (c, j // 2)], [ek], n)
+            acc("e" + c, e, T["Osk" if xs else "O16"][0:6, :], T.won[0:6, h], ["O16", "won" + c, "Osk"], [ek], n)
             for j in range(4):
-                mm(e, T.I16[:], pl(T.E, j), False, False, ["I16", "E%s%d" % (c, j // 2)], ["PM_e"], n)
-            mm(e, T.O16[0:4, :], T.won[0:4, h], False, False, ["O16", "won" + c], ["PM_e"], n)
-            for j in range(4):
-                mm(e, T.Im32[:], pl(T.Fd, j), False, j == 3, ["Im32", "Fd%s%d" % (c, j // 2)], ["PM_e"], n)
+                acc("e" + c, e, T["I16" if xs else "Im32"][:], pl(T.Fd, j), ["Im32", "Fd%s%d" % (c, j // 2), "I16"], [ek], n)
             x = 128 if last else 0
-            mm(dl, T.Nw[0:4, x:x + 128], T.won[0:4, h], False, True, ["Nw0", "Nw1", "won" + c], [dk], n)
-            act(T.U[:, h], e, F.Sigmoid, cf(5), LN2, ["PM_e", "cf5"], ["U" + c], n)
-            mm(T.PM[:, 256:256 + n], T.Ym[:], T.U[:, h], True, True, ["Ym", "U" + c], ["PM_y"], n)
-            if C["wins"][ch]:
-                act(T.win[:, h], T.PM[:, 256:256 + n], F.Sigmoid, -115.0, -9.0e28, ["PM_y"], ["win" + c], n)
+            acc("d" + c, dl, T.Nw[0:6, x:x + 128], T.won[0:6, h], ["Nw0", "won" + c, "Nw1"], [dk], n)
+            act(T.U[:, h], e, F.Sigmoid, cf(5), LN2, [ek, "cf5"], ["U" + c], n)
+            y = ey[:, 256:256 + n]
+            mm(y, T.Ym[:], T.U[:, h], True, True, ["Ym", "U" + c], [ek + "y"], n)
+            if C["wins"][ch] == "s":
+                act(T.win[:, h], y, F.Sigmoid, -115.0, -9.0e28, [ek + "y"], ["win" + c], n)
             else:
-                ts(T.win[:, h], T.PM[:, 256:256 + n], 0.0, None, A.is_lt, None, ["PM_y"], ["win" + c], n)
+                ts(T.win[:, h], y, 0.0, None, A.is_lt, None, [ek + "y"], ["win" + c], n)
             tt(td, T.win[:, h], dl, A.mult, ["win" + c, dk], [tk], n)
             if last:
                 tt(old, old, td, A.add, ok + [tk], ["Yf" + c], n)
@@ -626,55 +652,43 @@ def rank_program(g, core, T, topo):
                    ["Y%d" % u for u in range(4)] + ["Yf" + c], ["out" + c], 50.0, k="d", sem="st" + c, lat=3000.0)
                 wait("ys"[ch % 2], [], [], r=["out" + c])
             else:
-                gr = b // 128
-                x = 1024 * t + 512 * gr + 128 * rank + b % 128
-                tt(T.L[:, x:x + n], old, td, A.add, ok + [tk], ["L%d%d_%d" % (t, gr, b)], n)
-                if (b + n) % 128 == 0:
-                    sends.append(send(plan3, land(gr, rank, rank + 1), ["a%d_%d_%d" % (t, gr, rank)] * 3, "lsD", lkeys(gr),
-                                      C["gap"] if gr else 0.0))
+                tt(land(rank, b, n), old, td, A.add, ok + [tk], ["L%d%d" % (t, ch)], n)
+                if b + n in cuts:
+                    x = cuts.index(b + n)
+                    sends.append(send(plan3, land(rank, cuts[x - 1], b + n - cuts[x - 1]), ["a%d_%d_%d" % (t, x, rank)] * 3, "lsD",
+                                      ["L%d%d" % (t, y) for y in range(ch + 1)], C["gap"] if x > 1 else 0.0))
 
-        def lkeys(gr):
-            return ["L%d%d_%d" % (t, gr, p[0]) for p in ps if p[0] // 128 == gr]
+        def update():
+            def sem(x, r):
+                return ("a%d_%d_%d" % (t, x, r), len(e_near) if r == srank else hf)
 
-        def update(ch):
-            n = 128
-            lk = "L%d%d" % (t, ch)
-            tk = "T%d" % s
-            pg = (128 * ch, 128, ch, 2)
-
-            def sem(r):
-                return ("a%d_%d_%d" % (t, ch, r), len(e_near) if r == srank else hf)
-
-            if ch == 0:
-                wait("s", [sem(r) for r in range(4) if r != rank], [lk + "w"], after=[(sends[0], C["xch"]), (sends[1], 0.0)])
-                act(T.Tb[:, s:4096:8], land(0, 0, 4), F.Identity, 0.0, 1.0, lkeys(0) + [lk + "w", "ins"], [tk], 4 * n)
-                return
-            act(cols(T.Tb, rank, s, pg), land(ch, rank, rank + 1), F.Identity, 0.0, 1.0, lkeys(1) + ["ins"], [tk], n)
+            NS = len(cuts) - 1
+            b, n = cuts[-2], 256 - cuts[-2]
+            shift("s", cols(T.Tb, rank, s, 0, 256), land(rank, 0, 256), 0.0, ["L%d%d" % (t, ch) for ch in range(NP)] + ["ins"],
+                  ["T%d_%d" % (s, rank), "X%d_%d" % (s, rank)], 256)
+            for r in ([srank] + franks if b else []):
+                wk = "L%dw%d" % (t, r)
+                wait("s", [sem(x, r) for x in range(1, NS)], [wk], after=[(sends[-2], C["xch"]), (sends[-1], 0.0)])
+                shift("s", cols(T.Tb, r, s, 0, b), land(r, 0, b), 0.0, [wk], ["T%d_%d" % (s, r)], b)
             for e, r, l in (("s", srank, C["xch"] - 1000), ("v", franks[0], C["xch"]), ("s", franks[1], C["xch"])):
-                wk = lk + "w%d" % r
-                wait(e, [sem(r)], [wk], after=[(sends[ch], l)])
-                if e == "s":
-                    act(cols(T.Tb, r, s, pg), land(ch, r, r + 1), F.Identity, 0.0, 1.0, [wk, tk], ["X%d" % r], n)
-                else:
-                    op("v", lambda q, o=cols(T.Tb, r, s, pg), i=land(ch, r, r + 1): q.tensor_copy(o, i),
-                       [wk, tk], ["X%d" % r], dur(n))
+                wk = "L%dx%d" % (t, r)
+                wait(e, [sem(NS, r)], [wk], after=[(sends[-1], l)] + [(x, l + 1500.0) for x in sends[:-1]])
+                shift(e, cols(T.Tb, r, s, b, n), land(r, b, n), 0.0, [wk], ["X%d_%d" % (s, r)], n)
 
-        bs = [bcast(ch) for ch in range(NP)]
         for ch in range(NP):
-            head(ch, *bs[ch])
+            head(ch)
         for ch in range(NP):
             body(ch)
             if ch > 0:
                 tail(ch - 1)
         tail(NP - 1)
         if not last:
-            for ch in range(2):
-                update(ch)
-            nsent += 2 * (2 * hf + len(e_near))
+            update()
+            nsent += (len(cuts) - 1) * (2 * hf + len(e_near))
+            low[0] = -C["low"]
             prep(t + 1)
-            if t == 0:
-                TALL = TALL + ["X%d" % r for r in range(4)]
         if t in (1, 2, 3, 4):
             decode(t % 4)
+        low[0] = 0.0
     wait("g", [("lsD", nsent)], [], after=[(gq[0], 0.0)])
     _emit(g, T, ops)

import math
from concourse.bass import DstId, RemoteDMATransfer
from concourse.mybir import AluOpType, ActivationFunctionType

A = AluOpType
F = ActivationFunctionType
RO = 6
CFG = {
    "parts": [128, 128],
    "ks": [5, 5],
    "kc": [1, 1],
    "vw": [256, 256],
    "sw": [384, 384],
    "bvs": "vs",
    "wins": "sv",
    "fds": ["s", "sv"],
    "e1": [1, 0],
    "xs": [1, 0],
    "cuts": [0, 128, 256],
    "gap": 800.0, "xch": 3500.0, "low": 0.0,
    "cyc": 0.83, "pe": 0.42, "ovh": 30.0, "pov": 10.0, "gam": 1.56, "hop": 60.0,
}
PRIO = {}
CFG.update({"ks": [5, 4], "kc": [0, 1], "sw": [384, 256], "xch": 3200.0})
ORDER = [
    ("v", "Gb0 Gb1 Bv0 own0 Dv0_0 Dv0_2 Dv0_4 Dv0_6 Dv0_8 Dv0_10 Dv1_0 own1 Dv1_2 W0 Dv1_4 Q00 Q01 Q02 Q03 tes0 E00 "
          "Dv1_6 Dv1_8 Dv1_10 Cl1_10 W1 Q10 Q11 tes1 E10 Q12 Q13 E11 PW0t L0 f0 Fd11 nm win1 PW1t L1 f1 ph pt Sel cs Sv"),
    ("s", "G0_14 G0_11 Cl0_0 Bv1 Cl0_2 Cl0_4 Cl0_11 Cl0_6 Cl0_8 Cl0_14 Cl0_10 G1_12 Cl1_0 G1_14 Cl1_12 Cl1_2 Cl1_4 Cl1_14 "
          "Cl1_6 won0 Cl1_8 Fd00 U0 win0 Fd10 won1 U1 H00"),
    ("t", "PX_eyU1 PD0aTo1"), ("t", "PX_eyU1 PA000Cr00"), ("t", "PX_eyU1 PA110Cr10"),
]
BIG = 1.5 * 2.0 ** 27
MID = 32768.0
OFF = 24.5 / 16.0
LN2 = math.log(2.0)


def _sb(n, d):
    return ("sbuf", [128, n], d)


SCRATCH = {
    "Z": _sb(1024, "int32"), "Tb": _sb(4096, "float32"), "Yo": _sb(1024, "float32"), "L": _sb(5 * 1024, "float32"),
    "Dv": _sb(4096, "bfloat16"), "Cl": _sb(4096, "bfloat16"), "G": _sb(4096, "float32"),
    "Of": _sb(256, "uint16"), "Gb": _sb(256, "float16"), "Bv": _sb(1536, "float32"),
    "own": _sb(256, "bfloat16"), "W": _sb(256, "int32"),
    "Q": _sb(1024, "int32"), "E": _sb(1024, "bfloat16"), "tes": _sb(256, "bfloat16"), "won": _sb(256, "bfloat16"),
    "Fd": _sb(1024, "bfloat16"), "U": _sb(256, "bfloat16"), "win": _sb(256, "bfloat16"),
    "nm": _sb(256, "float16"), "Im1h": _sb(128, "float16"), "Ims": _sb(128, "bfloat16"), "Bw": _sb(512, "bfloat16"), "i1": _sb(1024, "int32"), "ph": _sb(256, "float16"),
    "pt": _sb(256, "float16"), "H": _sb(1024, "bfloat16"), "Sel": _sb(128 * RO, "float16"), "Sv": _sb(8 * RO, "float16"),
    "dn": _sb(256, "float16"),
    "xc": _sb(256, "float32"), "xg": _sb(128, "float32"), "pw": _sb(128, "float32"), "ci": _sb(16, "int32"),
    "cf": _sb(32, "float32"), "R64": _sb(144, "bfloat16"), "R16": _sb(144, "bfloat16"),
    "Imf": _sb(128, "float32"), "I16f": _sb(128, "float32"), "Im15": _sb(128, "float16"), "Im16": _sb(128, "float16"),
    "Im32": _sb(128, "bfloat16"), "I16": _sb(128, "bfloat16"), "I256": _sb(128, "bfloat16"),
    "I8k": _sb(128, "bfloat16"), "I1": _sb(128, "bfloat16"), "Im1": _sb(128, "bfloat16"), "Ym": _sb(128, "bfloat16"),
    "c2": _sb(128, "bfloat16"), "Pm": _sb(512, "float16"),
    "Om": _sb(128, "bfloat16"), "Ob": _sb(128, "bfloat16"), "O16": _sb(128, "bfloat16"), "O1": _sb(128, "bfloat16"),
    "Osk": _sb(128, "bfloat16"),
    "Nw": _sb(256, "bfloat16"), "Vw": _sb(16, "bfloat16"), "Vm": _sb(8, "bfloat16"), "vr": _sb(8, "float32"),
    "Iv": _sb(8, "bfloat16"), "xi": _sb(256, "bfloat16"), "Cr": _sb(1024, "bfloat16"),
}
for _n in ("PD0", "PD1", "PW0", "PW1", "PA0", "PA1", "PX", "PM"):
    SCRATCH[_n] = ("psum", [128, 512], "float32")
SEMAPHORES = (["ev", "es", "et", "eg", "lsI", "lsD", "arI"] + ["ld%d" % j for j in range(4)] + ["fw%d" % j for j in range(4)]
              + ["st%d" % j for j in range(4)]
              + ["a%d_%d_%d" % (t, p, r) for t in range(RO - 1) for p in range(4) for r in range(4)])
ESEM = {"v": "ev", "s": "es", "t": "et", "g": "eg"}


def _mask(engines):
    m = 0
    for e in engines:
        m |= 1 << e
    return m


def _deps(ops):
    lastw, readers, bank, deps, before = {}, {}, {}, [], {}
    for n, op in enumerate(ops):
        d = set()
        for k in op["r"]:
            d.update(lastw.get(k, []))
        grp = op.get("grp")
        if grp in before:
            d.update(before[grp])
            lastw[op["w"][0]].append(n)
            bank[op["w"][0][:3]][1].append(n)
        else:
            e = set()
            for k in op["w"]:
                e.update(lastw.get(k, []))
                e.update(readers.get(k, []))
            for k in set(k[:3] for k in op["r"] + op["w"] if k[0] == "P"):
                b = bank.setdefault(k, [None, [], []])
                if b[0] != op["e"]:
                    b[0], b[1], b[2] = op["e"], [], b[1]
                e.update(b[2])
                if op["e"] == "t":
                    e.update(b[1])
                b[1].append(n)
            if grp is not None:
                before[grp] = e
            d.update(e)
            for k in op["w"]:
                lastw[k] = [n]
                readers[k] = []
        if op["k"] != "r":
            for k in op["r"]:
                readers.setdefault(k, []).append(n)
        d.discard(n)
        deps.append(d)
    return deps


def _label(op):
    k = (op["w"] + op["r"] + ["-"])[0]
    if op["e"] == "t":
        k += op["r"][1]
    return op["e"] + (k[1:] if k[:2] == "Yf" else k[0] + k[2:] if k[0] in "LTXY" else k)


def _order(ops, deps):
    n = len(ops)
    succ = [[] for _ in range(n)]
    edges = [[(m, 0.0 if ops[m]["k"] == "w" or (ops[m]["e"] == "t" and ops[i]["e"] == "t") else ops[m]["lat"]) for m in deps[i]]
             + list(ops[i]["after"]) for i in range(n)]
    named = {(o["rd"], _label(o)): i for i, o in enumerate(ops)}
    for t in range(RO):
        for e, names in ORDER:
            row = [named[(t, e + x)] for x in names.split() if (t, e + x) in named]
            for m, i in zip(row, row[1:]):
                edges[i].append((m, 0.0))
    for i in range(n):
        for m, l in edges[i]:
            succ[m].append((i, l))
    pr = [0.0] * n
    left = [len(e) for e in edges]
    topo_ = [i for i in range(n) if left[i] == 0]
    for i in topo_:
        for j, l in succ[i]:
            left[j] -= 1
            if left[j] == 0:
                topo_.append(j)
    assert len(topo_) == n
    for i in reversed(topo_):
        pr[i] = ops[i]["d"] + max([l + pr[j] for j, l in succ[i]] + [0.0])
    for i in range(n):
        pr[i] += PRIO.get(_label(ops[i]), 0) + ops[i]["p"]
    left = [len(e) for e in edges]
    rdy = [0.0] * n
    free = {}
    ready = {}
    for i in range(n):
        if left[i] == 0:
            ready.setdefault(ops[i]["e"], []).append(i)
    order = []
    while len(order) < n:
        best = None
        for e, l in ready.items():
            if l:
                t0 = max(free.get(e, 0.0), min(rdy[i] for i in l))
                if best is None or t0 < best[0]:
                    best = (t0, e)
        t0, e = best
        cand = [i for i in ready[e] if rdy[i] <= t0 + 1e-6]
        i = max(cand, key=lambda j: (pr[j], -j))
        soon = [j for j in ready[e] if t0 < rdy[j] < t0 + 0.5 * ops[i]["d"] and pr[j] > pr[i] + ops[i]["d"]]
        if soon:
            i = min(soon, key=lambda j: rdy[j])
            t0 = rdy[i]
        ready[e].remove(i)
        order.append(i)
        free[e] = t0 + ops[i]["d"]
        for j, l in succ[i]:
            rdy[j] = max(rdy[j], free[e] + l)
            left[j] -= 1
            if left[j] == 0:
                ready.setdefault(ops[j]["e"], []).append(j)
    return order, max(free.values())


def _emit(g, T, ops):
    qs = {"v": g.vector, "s": g.scalar, "t": g.tensor, "g": g, "y": g.sync}
    deps = _deps(ops)
    order = _order(ops, deps)[0]
    pos = {i: p for p, i in enumerate(order)}
    seen, waits, members = {}, {}, {}
    for i in order:
        members.setdefault(ops[i].get("grp"), []).append(i)
    for i in order:
        op, best = ops[i], {}
        for m in deps[i]:
            o = ops[m]
            if o["k"] in "wr" or (o["e"] == "t" and op["e"] == "t"):
                continue
            key = o["e"] if o["k"] == "c" else m
            if key not in best or pos[best[key]] < pos[m]:
                best[key] = m
        waits[i] = []
        for key, m in best.items():
            if seen.get((op["e"], key), -1) < pos[m]:
                seen[(op["e"], key)] = pos[m]
                waits[i].append(m)
    need = set(m for w in waits.values() for m in w)
    count, val = {}, {}
    for i in order:
        op = ops[i]
        if op["k"] == "c" and i in need:
            count[op["e"]] = count.get(op["e"], 0) + 1
            val[i] = (ESEM[op["e"]], count[op["e"]])
        elif op["k"] == "d":
            val[i] = (op["sem"], 16)
    for i in order:
        op = ops[i]
        q = qs[op["e"]]
        for m in waits[i]:
            q.wait_ge(T.sem[val[m][0]], val[m][1])
        if op["k"] == "w":
            for s, v in op["sems"]:
                q.wait_ge(T.sem[s], v)
            continue
        if op.get("grp") is None:
            ins = op["f"](q)
        else:
            ins = op["f"](q, members[op["grp"]][0] == i, members[op["grp"]][-1] == i)
        if i in val:
            ins.then_inc(T.sem[val[i][0]], 16 if op["k"] == "d" else 1)


def _helper(T, topo, core):
    other = [c for c in T.cores if topo.chip(c) != topo.chip(core)][0]
    return [c for c in topo.cores_of(other)
            if T.rank_of(c) is None and topo.die(c) == topo.die(core) and topo.may_write(core, c)][0]


def _hand_on(g, core, T, topo):
    for src in T.cores:
        if _helper(T, topo, src) != core:
            continue
        r = T.rank_of(src)
        to = [c for c in T.cores if topo.chip(c) == topo.chip(core)]
        es = topo.engines(core, to[0])
        k = len(es) // len(to)
        for j in range(4):
            ap = T.Tb[:, 1024 * r + 256 * j:1024 * r + 256 * j + 256]
            g.wait_ge(T.sem["fw%d" % j], len(topo.engines(src, core)))
            g.remote_dma_fused([RemoteDMATransfer(dst_ids=[DstId(rid=topo.addr(c)[0], pnc=topo.addr(c)[1])],
                                                  dma_engine_mask=_mask(es[k * x:k * x + k]), remote_sem=T.sem.arI, src=ap, dst=ap)
                                for x, c in enumerate(to)], local_sem=T.sem.lsI)
        g.wait_ge(T.sem.lsI, 4 * len(es))


def rank_program(g, core, T, topo):
    rank = T.rank_of(core)
    if rank is None:
        _hand_on(g, core, T, topo)
        return
    C = CFG
    NP = len(C["parts"])
    cuts = C["cuts"]
    others = [c for c in T.cores if c != core]
    sib = [c for c in others if topo.chip(c) == topo.chip(core)][0]
    far = [c for c in others if topo.chip(c) != topo.chip(core)]
    peer = [c for c in far if topo.die(c) == topo.die(core)][0]
    e_far = topo.engines(core, peer)
    e_all = topo.engines(core, sib)
    e_near = [e for e in e_all if e not in e_far]
    hf = len(e_far) // 2
    plan3 = [(far[0], e_far[:hf]), (far[1], e_far[hf:]), (sib, e_near)]
    srank = T.rank_of(sib)
    franks = [T.rank_of(c) for c in far]
    ops = []
    low = [0.0]
    rd = [-1]

    def op(e, f, r, w, d, k="c", lat=None, after=(), **kw):
        o = {"e": e, "f": f, "r": list(r), "w": list(w), "k": k, "d": d, "lat": C["hop"] if lat is None else lat,
             "after": list(after), "p": low[0], "rd": rd[0]}
        o.update(kw)
        ops.append(o)
        return len(ops) - 1

    def wait(e, sems, w, after=(), r=()):
        return op(e, None, r, w, 0.0, k="w", sems=sems, after=after)

    def dur(n, gth=False):
        return 55.0 + n * C["gam"] * C["cyc"] if gth else max(64.0, n) * C["cyc"] + C["ovh"]

    def ts(out, in0, s1, s2, o0, o1, r, w, n, gth=False):
        if s2 is None:
            op("v", lambda q: q.tensor_scalar(out, in0, s1, None, o0), r, w, dur(n, gth))
        else:
            op("v", lambda q: q.tensor_scalar(out, in0, s1, s2, o0, o1), r, w, dur(n, gth))

    def tt(out, a, b, o, r, w, n, gth=False):
        op("v", lambda q: q.tensor_tensor(out, a, b, o), r, w, dur(n, gth))

    def act(out, in_, fn, bias, scale, r, w, n, gth=False):
        op("s", lambda q: q.activation(out, in_, fn, bias=bias, scale=scale), r, w, dur(n, gth))

    def shift(e, out, in_, c, r, w, n):
        if e == "s":
            act(out, in_, F.Identity, c, 1.0, r, w, n)
        else:
            ts(out, in_, c, None, A.add, None, r, w, n)

    def fill(out, c, w):
        op("v", lambda q: q.memset(out, c), [], w, 83.0)

    def mm(out, lhsT, rhs, start, stop, r, w, n, f32=False):
        op("t", lambda q: q.matmul(out, lhsT, rhs, start, stop), r, w, max(64, n) * (4 if f32 else 1) * C["pe"] + C["pov"], lat=C["hop"] + 45)

    def acc(grp, out, lhsT, rhs, r, w, n):
        op("t", lambda q, start, stop: q.matmul(out, lhsT, rhs, start, stop), r, w, max(64, n) * C["pe"] + C["pov"],
           lat=C["hop"] + 45, grp=grp + str(rd[0]))

    def iota(out, pat, base, cm, w, n, flt=True):
        if flt:
            op("g", lambda q: q.iota(out, pat, base, cm, allow_small_or_imprecise_dtypes=True), [], w, 130 + 2 * n * C["cyc"])
        else:
            op("g", lambda q: q.iota(out, pat, base, cm), [], w, 130 + 2 * n * C["cyc"])

    def dst(c):
        a = topo.addr(c)
        return DstId(rid=a[0], pnc=a[1])

    gq = [None]

    def send(plan, ap, rsems, lsem, r, gap=0.0):
        tr = [RemoteDMATransfer(dst_ids=[dst(c)], dma_engine_mask=_mask(es), remote_sem=T.sem[rs], src=ap, dst=ap)
              for (c, es), rs in zip(plan, rsems)]
        gq[0] = op("g", lambda q: q.remote_dma_fused(tr, local_sem=T.sem[lsem]), r, [], 500.0, k="r",
                   after=[(gq[0], gap)] if gq[0] is not None else [])
        return gq[0]

    ps, b0 = [], 0
    for n in C["parts"]:
        ps.append((b0, n))
        b0 += n

    for j in range(4):
        op("ys"[j % 2], lambda q, j=j: q.dma_start(T.Z[:, 256 * j:256 * j + 256], T.kin[:, 256 * j:256 * j + 256]),
           [], ["Z%d" % j], 50.0, k="d", sem="ld%d" % j, lat=2200.0 + 300 * j)
    iota(T.ci[:, 0:1], [[0, 1]], 0, 1, ["ci0"], 1, flt=False)
    iota(T.xc[:], [[1, 256]], 0, 0, ["xc"], 256)
    iota(T.pw[:], [[0, 128]], 0, 1, ["pw"], 128)
    iota(T.xg[:], [[16, 8], [0, 16]], 0, 0, ["xg"], 128)
    fill(T.Vw[:], 0.0, ["Vw"])
    fill(T.Vw[:, 3:4], 2.0, ["Vw"])
    fill(T.Vm[:], 0.0, ["Vm"])
    fill(T.Vm[:, 0:4], -1.0, ["Vm"])
    fill(T.vr[:], 0.0, ["vr"])
    fill(T.vr[:, 4:5], 1.0, ["vr"])
    fill(T.vr[:, 5:6], -1.0, ["vr"])

    def ci(j):
        return T.ci[:, j:j + 1]

    def cf(j):
        return T.cf[:, j:j + 1]

    for j, m in ((1, 112), (2, 16), (3, 15), (4, 1), (5, 2)):
        ts(ci(j), ci(0), m, None, A.bitwise_and, None, ["ci0"], ["ci%d" % j], 1)
    ts(cf(0), ci(0), 0.0, None, A.add, None, ["ci0"], ["cf0"], 1)
    ts(cf(1), ci(1), 15.0, None, A.add, None, ["ci1"], ["cf1"], 1)
    ts(cf(2), ci(1), 0.0, None, A.add, None, ["ci1"], ["cf2"], 1)
    ts(cf(3), ci(2), 62.5, cf(0), A.mult, A.add, ["ci2", "cf0"], ["cf3"], 1)
    ts(cf(4), ci(2), -62.5, cf(0), A.mult, A.add, ["ci2", "cf0"], ["cf4"], 1)
    ts(cf(5), ci(3), -LN2, -LN2 * 1354.0, A.mult, A.add, ["ci3"], ["cf5"], 1)
    ts(cf(6), ci(5), 1.5, 1.0, A.mult, A.add, ["ci5"], ["cf6"], 1)
    ts(cf(7), ci(4), 1.0, cf(6), A.add, A.mult, ["ci4", "cf6"], ["cf7"], 1)
    act(cf(9), cf(0), F.Sigmoid, -3.5 * 256.0, 256.0, ["cf0"], ["cf9"], 1)
    ts(cf(10), cf(9), -1.0, 1.0, A.mult, A.add, ["cf9"], ["cf10"], 1)
    ts(cf(11), cf(9), 192.0, None, A.mult, None, ["cf9"], ["cf11"], 1)
    ts(cf(12), cf(7), cf(10), cf(11), A.mult, A.add, ["cf7", "cf10", "cf11"], ["cf12"], 1)
    ts(cf(8), cf(12), 0.0625, None, A.mult, None, ["cf12"], ["cf8"], 1)
    ts(cf(13), cf(9), 1008.0, 16.0, A.mult, A.add, ["cf9"], ["cf13"], 1)
    ts(cf(15), cf(9), 1024.0, None, A.mult, None, ["cf9"], ["cf15"], 1)
    ts(cf(14), ci(4), 2.0, -1.0, A.mult, A.add, ["ci4"], ["cf14"], 1)
    ts(cf(14), cf(14), cf(9), None, A.mult, None, ["cf14", "cf9"], ["cf14"], 1)
    for s in range(4):
        ts(cf(16 + s), cf(14), 256.0 * (16.0 * (1024 * rank + s) - MID), -128.0, A.mult, A.add, ["cf14"], ["cw%d" % s], 1)
    x128 = T.xc[:, 0:128]
    for c in range(2):
        for gm in range(2):
            sh = -16.0 * gm if c == 0 else -16.0 * (gm - 1) - 1000.0
            j = 2 * c + gm
            ts(T.Pm[:, 128 * j:128 * j + 128], x128, sh, cf(3 + c), A.add, A.is_equal, ["xc", "cf3", "cf4"], ["cPm%d" % j], 128)
    for nm, wgt in (("Imf", -1.0), ("Im15", -15.0), ("Im16", -16.0), ("Im1h", -1.0)):
        ts(T[nm][:], x128, cf(0), wgt, A.is_equal, A.mult, ["xc", "cf0"], [nm], 128)
    for nm, wgt, c in (("I8k", 8192.0, 0.0), ("I16", 16.0, 0.0), ("I256", 256.0, 0.0), ("I16f", 16.0, 0.0), ("Im32", -32.0, 0.0),
                       ("I1", 1.0, 0.0), ("Im1", -1.0, 0.0), ("Ims", -0.0625, 0.0), ("Ob", 49152.0, 512.0),
                       ("Om", 0.0, -256.0), ("O1", 0.0, 1.0)):
        act(T[nm][:], T.Imf[:], F.Identity, c, -wgt, ["Imf"], [nm], 128)
    ts(T.R64[:], T.xc[:, 0:144], cf(1), 64.0, A.is_equal, A.mult, ["xc", "cf1"], ["R64"], 144)
    act(T.R16[:], T.R64[:], F.Identity, 0.0, 0.25, ["R64"], ["R16"], 144)
    ts(T.c2[:], T.xg[:], cf(2), None, A.is_equal, None, ["xg", "cf2"], ["c2"], 128)
    op("g", lambda q: q.affine_select(T.Ym[:], T.c2[:], [[-1, 128]], A.not_equal, -1.0, 0, 1), ["c2"], ["Ym"], 400.0)
    for o, j, k in ((T.Nw[:, 0:128], 8, "Nw0"), (T.Nw[:, 128:256], 12, "Nw1"), (T.O16[:], 13, "O16"), (T.Osk[:], 15, "Osk")):
        act(o, T.pw[:], F.Identity, cf(j), 0.0, ["pw", "cf%d" % j], [k], 128)
    for j in range(4):
        ts(T.Bw[:, 128 * j:128 * j + 128], T.pw[:], float(j), -1.0, A.is_equal, A.mult, ["pw"], ["Bw%d" % j], 128)
    act(T.Iv[:], T.vr[:], F.Identity, 0.0, -64.0, ["vr"], ["Iv"], 8)
    act(T.xi[:], T.xc[:], F.Identity, 0.0, 1.0, ["xc"], ["xi"], 256)
    for ch, (b, n) in enumerate(ps):
        for j in range(4):
            act(T.Cr[0:32, 4 * b + n * j:4 * b + n * j + n], T.xc[0:32, 0:n], F.Identity,
                32.0 + 2 ** j + (1536.0 if j == 3 else -192.0 * 2 ** j), 0.0, ["xc"], ["Cr%d%d" % (ch, j)], n)

    PDk = [(T.PD0, "PD0"), (T.PD1, "PD1")]
    OWN = ["To%d" % j for j in range(4)]
    for j in range(4):
        pb, pk = PDk[j % 2]
        low[0] = 1000.0 * (4 - j)
        zs, cs = T.Z[:, 256 * j:256 * j + 256], T.Tb[:, 1024 * rank + 256 * j:1024 * rank + 256 * j + 256]
        i1 = T.i1[:, 256 * j:256 * j + 256]
        ts(i1, zs, 15, None, A.bitwise_and, None, ["Z%d" % j], ["i1%d" % j], 256)
        ts(pb[:, 0:256], i1, -0.9375, None, A.mult, None, ["i1%d" % j], [pk + "a"], 256)
        tt(cs, zs, pb[:, 0:256], A.add, ["Z%d" % j, pk + "a"], [OWN[j]], 256)
        send([(_helper(T, topo, core), e_far), (sib, e_near)], cs, ["fw%d" % j, "arI"], "lsI", [OWN[j]])
    low[0] = 0.0
    for e in "vs":
        wait(e, [("arI", 4 * (len(e_near) + len(e_all))), ("lsI", 4 * len(e_all))], ["in" + e], after=[(gq[0], 9000.0)])

    PA = [(T.PA0, "PA0"), (T.PA1, "PA1")]
    PW = [(T.PW0, "PW0"), (T.PW1, "PW1")]

    def tkeys(s):
        return OWN + ["T%d_%d" % (s, rank), "X%d_%d" % (s, rank)]

    def cols(buf, r, s, b, n):
        c0 = 1024 * r + 4 * b + s
        return buf[:, c0:c0 + 4 * (n - 1) + 1:4]

    def prep(t):
        s = t % 4
        tk = tkeys(s)
        u = cols(T.Tb, rank, s, 0, 256)
        ts(T.Sel[:, 128 * t:128 * t + 128], T.pw[:], float(17 * t + 3), None, A.is_equal, None, ["pw"], ["Sel", "Sel%d" % t], 128)
        ts(cf(20 + t), cf(0), float(17 * t + 3), None, A.is_equal, None, ["cf0"], ["cs", "cs%d" % t], 1)
        ts(T.Sv[:, 8 * t:8 * t + 8], T.vr[:], cf(20 + t), None, A.mult, None, ["vr", "cs%d" % t], ["Sv", "Sv%d" % t], 8)
        ts(T.ph[:], u, 0.0625, -2048.0, A.mult, A.add, tk, ["ph"], 256)
        op("v", lambda q: q.transpose(T.pt[:], T.ph[:]), ["ph"], ["pt"], dur(128))
        for ch, (b, n) in enumerate(ps):
            nh = n // 16
            for bb in range(n // 32):
                for c in range(2):
                    o = b + 2 * bb + c
                    for gm in range(2):
                        j = 2 * c + gm
                        x = b + 32 * bb + 16 * gm
                        mm(T.PX[:, o:o + 15 * nh + 1:nh], T.Pm[:, 128 * j:128 * j + 128], T.pt[:, x:x + 16], gm == 0, gm == 1,
                           ["cPm%d" % j, "pt"], ["PX_o"], 16)
        ts(T.Of[:], T.PX[:, 0:256], 2048.0, None, A.add, None, ["PX_o"], ["Of"], 256)
        ts(T.nm[:], u, BIG, -BIG - MID, A.add, A.add, tk, ["nm"], 256)
        mm(T.PD0[:, 0:256], T.I16f[:], u, True, False, tk + ["I16f"], ["PD0a"], 256, True)
        mm(T.PD0[:, 0:256], T.Im16[:], T.nm[:], False, True, ["nm", "Im16"], ["PD0a"], 256)
        for ch, (b, n) in enumerate(ps):
            pa, pk = PA[(4 * b) // 512]
            x = 4 * b % 512
            hk = ["H%d%d" % (ch, j) for j in range(4)]
            ak = [pk + "%d%d" % (ch, j) for j in range(4)]
            for j in range(4):
                act(T.H[:, 4 * b + n * j:4 * b + n * j + n], T.PD0[:, b:b + n], F.Identity,
                    192.0 * 2 ** j - (2 ** j - 1) / 2.0 - 16.0 * MID, 1.0, ["PD0a"], [hk[j]], n)
            mm(pa[:, x:x + 4 * n], T.O1[0:1, :], T.Cr[0:1, 4 * b:4 * b + 4 * n], True, False,
               ["O1"] + ["Cr%d%d" % (ch, j) for j in range(4)], ak, 4 * n)
            mm(pa[:, x:x + 3 * n], T.I1[:], T.H[:, 4 * b + n:4 * b + 4 * n], False, False, ["I1"] + hk, ak, 3 * n)
            mm(pa[:, x:x + 4 * n], T.Im1[:], T.H[:, 4 * b:4 * b + 4 * n], False, True, ["Im1"] + hk, ak, 4 * n)

    def decode(s):
        tk = tkeys(s)
        u = cols(T.Tb, rank, s, 0, 256)
        ts(T.dn[:], u, BIG, -BIG - MID, A.add, A.add, tk, ["dn"], 256)
        mm(T.PD1[:, 0:256], T.I16f[:], u, True, False, tk + ["I16f"], ["PD1a"], 256, True)
        mm(T.PD1[:, 0:256], T.Im15[:], T.dn[:], False, True, ["dn", "Im15"], ["PD1a"], 256)
        act(T.Yo[:, s:1024:4], T.PD1[:, 0:256], F.Identity, -15.0 * MID, 1.0, ["PD1a"], ["Y%d" % s], 256)

    prep(0)
    win_all = T.Tb[:, 0:4096]
    TALL = OWN + [k + "%d_%d" % (s, r) for k in "TX" for s in range(4) for r in range(4)]
    pdn = [0]
    nsent = 0

    for t in range(RO):
        s = t % 4
        last = t == RO - 1
        sel, selk = T.Sel[:, 128 * t:128 * t + 128], "Sel%d" % t
        sends = []
        rd[0] = t

        def head(ch):
            b, n = ps[ch]
            h = slice(b, b + n)
            c = str(ch)
            nh = n // 16
            vw = C["vw"][ch]
            bp, bk = [(T.PX, "PX_b0"), (T.PM, "PM_b1"), (T.PX, "PX_b2")][ch]
            x = 256 if ch == 2 else 0
            ts(T.Gb[:, h], win_all.indirect(T.Of[:, b + nh * t:b + nh * (t + 1)]), BIG, -BIG - MID, A.add, A.add,
               TALL + ["Of", "inv"], ["Gb" + c], n, True)
            for u in range(vw // n):
                mm(bp[:, x + n * u:x + n * u + n], sel, T.Gb[:, h], True, True, [selk, "Gb" + c], [bk], n)
            shift(C["bvs"][ch], T.Bv[:, 512 * ch:512 * ch + vw], bp[:, x:x + vw], MID - OFF, [bk], ["Bv" + c], vw)
            tt(T.own[:, h], T.nm[:, h], bp[:, x:x + n], A.is_equal, ["nm", bk], ["own" + c], n)

        def body(ch):
            b, n = ps[ch]
            h = slice(b, b + n)
            nh = n // 16
            c = str(ch)
            pw_, wk = PW[ch % 2]
            kk = C["vw"][ch] // n
            nks = C["ks"][ch]

            def gath(k, m):
                return win_all.indirect(T.Of[:, b + nh * k:b + nh * (k + m)])

            def sl(k, m=1):
                return slice(16 * b + n * k, 16 * b + n * (k + m))

            red = []
            k = 16 - nks
            while k < 16:
                m = min(C["sw"][ch] // n, 16 - k)
                pb, pk = PDk[pdn[0] % 2]
                pdn[0] += 1
                act(T.G[:, sl(k, m)], gath(k, m), F.Identity, 0.0, 1.0, TALL + ["Of", "ins"], ["G%s_%d" % (c, k)], n * m, True)
                mm(pb[:, 0:n * m], T.Imf[:], T.G[:, sl(k, m)], True, False, ["Imf", "G%s_%d" % (c, k)], [pk + "a"], n * m, True)
                for u in range(m):
                    mm(pb[:, n * u:n * u + n], sel, T.Gb[:, h], False, u == m - 1, [selk, "Gb" + c], [pk + "a"], n)
                act(T.Cl[:, sl(k, m)], pb[:, 0:n * m], F.Sigmoid, OFF - 2.0 - MID, -1.0, [pk + "a"],
                    ["Cl%s_%d" % (c, k + u) for u in range(m)], n * m)
                red.append([(k + u, "R64") for u in range(m)])
                k += m
            vred = []
            ks = list(range(0, 16 - nks, kk))
            for x, k in enumerate(ks):
                m = (ks + [16 - nks])[x + 1] - k
                dk = "Dv%s_%d" % (c, k)
                tt(T.Dv[:, sl(k, m)], gath(k, m), T.Bv[:, 512 * ch:512 * ch + n * m], A.subtract,
                   TALL + ["Of", "inv", "Bv" + c], [dk], n * m, True)
                w = ["Cl%s_%d" % (c, k + u) for u in range(m)]
                mine = x >= len(ks) - C["kc"][ch]
                if mine:
                    ts(T.Cl[:, sl(k, m)], T.Dv[:, sl(k, m)], 0.0, 4.0, A.max, A.min, [dk], w, n * m / 2)
                else:
                    act(T.Cl[:, sl(k, m)], T.Dv[:, sl(k, m)], F.Sigmoid, -2.0, 1.0, [dk], w, n * m)
                vred.append([(k + u, "R16" if mine else "R64") for u in range(m)])
            acc("w" + c, pw_[:, 0:n], T.I8k[:], T.own[:, h], ["I8k", "own" + c], [wk + "w"], n)
            for k, R in sum(red + vred, []):
                acc("w" + c, pw_[:, 0:n], T[R][:, 15 - k:143 - k], T.Cl[:, sl(k)], [R, "Cl%s_%d" % (c, k)], [wk + "w"], n)

        def land(r, b, n):
            x = 1024 * t + 256 * r + b
            return T.L[:, x:x + n]

        def tail(ch):
            b, n = ps[ch]
            h = slice(b, b + n)
            c = str(ch)
            pw_, wk = PW[ch % 2]
            pa, pk = PA[(4 * b) // 512]
            old, ok = (cols(T.Yo, 0, s, b, n), ["Y%d" % s]) if last else (cols(T.Tb, rank, s, b, n), tkeys(s))

            def pl(buf, j, m=1):
                return buf[:, 4 * b + n * j:4 * b + n * (j + m)]

            ts(T.W[:, h], pw_[:, 0:n], 7.5, 2080.0, A.add, A.min, [wk + "w"], ["W" + c], n)
            dl, dk, td, tk = pw_[:, 128:128 + n], wk + "n", pw_[:, 384:384 + n], wk + "t"
            free = ch == NP - 1 or (4 * ps[ch + 1][0]) // 512 != (4 * b) // 512
            ey, ek = (pa, pk + "e") if free else (T.PM, "PM_e")
            if ch == NP - 1:
                ey, ek = T.PX, "PX_e"
            if ch + 2 < NP:
                dl, dk, td, tk = pa[:, 0:n], pk + "n", pa[:, 384:384 + n], pk + "t"
                ey, ek = T.PM, "PM_e"

            def delta():
                acc("d" + c, dl, sel, T.Gb[:, h], [selk, "Gb" + c], [dk], n)
                acc("d" + c, dl, T.Im1h[:], T.nm[:, h], ["Im1h", "nm"], [dk], n)
                acc("d" + c, dl, T["Im1" if last else "Ims"][:], pl(T.H, 0), ["Ims", "H%s0" % c, "Im1"], [dk], n)

            if ch + 2 >= NP:
                delta()
            for j in range(4):
                ts(pl(T.Q, j), T.W[:, h], 32 + (1 << j), None, A.bitwise_and, None, ["W" + c], ["Q%s%d" % (c, j)], n)
            ts(T.tes[:, h], pl(T.Q, 0), 32.0, None, A.is_ge, None, ["Q%s0" % c], ["tes" + c], n)
            vb, vk = T.PM[0:6, 0:n], "PM_v"
            acc("v" + c, vb, T.Sv[:, 8 * t:8 * t + 6], T.Gb[:, h], ["Sv%d" % t, "Gb" + c], [vk], n)
            acc("v" + c, vb, T.Iv[0:1, 0:6], T.xi[0:1, h], ["Iv", "xi"], [vk], n)
            acc("v" + c, vb, T.Vm[:, 0:6], T.tes[:, h], ["Vm", "tes" + c], [vk], n)
            split = len(C["fds"][ch]) == 2
            xs = C["xs"][ch]
            xb = [(T.PD0, "PD0a", 0), (T.PD1, "PD1a", 0)] if split else [(T.PX, "PX_x", 0), (T.PX, "PX_x", 2 * n)]
            for u in range(2):
                x = (4 * b + 2 * n * u) % 512
                if not C["e1"][ch]:
                    tt(pl(T.E, 2 * u, 2), pl(T.Q, 2 * u, 2), pa[:, x:x + 2 * n], A.is_equal,
                       ["Q%s%d" % (c, 2 * u + j) for j in range(2)] + [pk + "%d%d" % (ch, 2 * u + j) for j in range(2)],
                       ["E%s%d" % (c, u)], 2 * n)
                elif u == 0:
                    tt(pl(T.E, 0, 4), pl(T.Q, 0, 4), pa[:, x:x + 4 * n], A.is_equal,
                       ["Q%s%d" % (c, j) for j in range(4)] + [pk + "%d%d" % (ch, j) for j in range(4)],
                       ["E%s0" % c, "E%s1" % c], 4 * n)
                for j in range(2):
                    o = xb[u][0][:, xb[u][2] + n * j:xb[u][2] + n * j + n]
                    if not xs:
                        mm(o, T.Om[:], T.tes[:, h], True, False, ["Om", "tes" + c], [xb[u][1]], n)
                        mm(o, T.Ob[:], pl(T.E, 2 * u + j), False, True, ["Ob", "E%s%d" % (c, u)], [xb[u][1]], n)
            for j in range(4):
                acc("v" + c, vb, T.Vw[:, 3 - j:9 - j], pl(T.E, j), ["Vw", "E%s%d" % (c, j // 2)], [vk], n)
            act(T.won[0:6, h], vb, F.Sigmoid, T.cf[0:6, 16 + s:17 + s], 256.0, [vk, "cw%d" % s], ["won" + c], n)
            for u in range((2 if split else 1) if xs else 0):
                m = 2 if split else 4
                mm(xb[u][0][:, 0:m * n], T.I1[:], pl(T.E, m * u, m), True, False,
                   ["I1"] + ["E%s%d" % (c, x) for x in ([u] if split else [0, 1])], [xb[u][1]], m * n)
                for j in range(m):
                    mm(xb[u][0][:, n * j:n * j + n], T.Bw[0:4, 128 * (m * u + j):128 * (m * u + j + 1)], T.won[0:4, h], False, j == m - 1,
                       ["Bw%d" % (m * u + j), "won" + c], [xb[u][1]], n)
            for u, e in enumerate(C["fds"][ch]):
                m = 2 if split else 4
                o, i, r, w = pl(T.Fd, m * u, m), xb[u][0][:, 0:m * n], [xb[u][1]], ["Fd%s%d" % (c, x) for x in ([u] if split else [0, 1])]
                if e == "s":
                    act(o, i, F.Abs if xs else F.Sigmoid, 0.0 if xs else -49280.0, 1.0, r, w, m * n)
                else:
                    ts(o, i, 0.0 if xs else 49280.0, None, A.not_equal if xs else A.is_gt, None, r, w, m * n)
            if ch + 2 < NP:
                delta()
            e = ey[:, 128:128 + n]
            acc("e" + c, e, T.I256[:], T.tes[:, h], ["I256", "tes" + c], [ek], n)
            acc("e" + c, e, T.I256[:], T.own[:, h], ["I256", "own" + c], [ek], n)
            for j in range(0 if xs else 4):
                acc("e" + c, e, T.I16[:], pl(T.E, j), ["I16", "E%s%d" % (c, j // 2)], [ek], n)
            acc("e" + c, e, T["Osk" if xs else "O16"][0:6, :], T.won[0:6, h], ["O16", "won" + c, "Osk"], [ek], n)
            for j in range(4):
                acc("e" + c, e, T["I16" if xs else "Im32"][:], pl(T.Fd, j), ["Im32", "Fd%s%d" % (c, j // 2), "I16"], [ek], n)
            x = 128 if last else 0
            acc("d" + c, dl, T.Nw[0:6, x:x + 128], T.won[0:6, h], ["Nw0", "won" + c, "Nw1"], [dk], n)
            act(T.U[:, h], e, F.Sigmoid, cf(5), LN2, [ek, "cf5"], ["U" + c], n)
            y = ey[:, 256:256 + n]
            mm(y, T.Ym[:], T.U[:, h], True, True, ["Ym", "U" + c], [ek + "y"], n)
            if C["wins"][ch] == "s":
                act(T.win[:, h], y, F.Sigmoid, -115.0, -9.0e28, [ek + "y"], ["win" + c], n)
            else:
                ts(T.win[:, h], y, 0.0, None, A.is_lt, None, [ek + "y"], ["win" + c], n)
            tt(td, T.win[:, h], dl, A.mult, ["win" + c, dk], [tk], n)
            if last:
                tt(old, old, td, A.add, ok + [tk], ["Yf" + c], n)
                op("ys"[ch % 2], lambda q: q.dma_start(T.yk[:, 4 * b:4 * b + 4 * n], T.Yo[:, 4 * b:4 * b + 4 * n]),
                   ["Y%d" % u for u in range(4)] + ["Yf" + c], ["out" + c], 50.0, k="d", sem="st" + c, lat=3000.0)
                wait("ys"[ch % 2], [], [], r=["out" + c])
            else:
                tt(land(rank, b, n), old, td, A.add, ok + [tk], ["L%d%d" % (t, ch)], n)
                if b + n in cuts:
                    x = cuts.index(b + n)
                    sends.append(send(plan3, land(rank, cuts[x - 1], b + n - cuts[x - 1]), ["a%d_%d_%d" % (t, x, rank)] * 3, "lsD",
                                      ["L%d%d" % (t, y) for y in range(ch + 1)], C["gap"] if x > 1 else 0.0))

        def update():
            def sem(x, r):
                return ("a%d_%d_%d" % (t, x, r), len(e_near) if r == srank else hf)

            NS = len(cuts) - 1
            b, n = cuts[-2], 256 - cuts[-2]
            shift("s", cols(T.Tb, rank, s, 0, 256), land(rank, 0, 256), 0.0, ["L%d%d" % (t, ch) for ch in range(NP)] + ["ins"],
                  ["T%d_%d" % (s, rank), "X%d_%d" % (s, rank)], 256)
            for r in ([srank] + franks if b else []):
                wk = "L%dw%d" % (t, r)
                wait("s", [sem(x, r) for x in range(1, NS)], [wk], after=[(sends[-2], C["xch"]), (sends[-1], 0.0)])
                shift("s", cols(T.Tb, r, s, 0, b), land(r, 0, b), 0.0, [wk], ["T%d_%d" % (s, r)], b)
            for e, r, l in (("s", srank, C["xch"] - 1000), ("v", franks[0], C["xch"]), ("s", franks[1], C["xch"])):
                wk = "L%dx%d" % (t, r)
                wait(e, [sem(NS, r)], [wk], after=[(sends[-1], l)] + [(x, l + 1500.0) for x in sends[:-1]])
                shift(e, cols(T.Tb, r, s, b, n), land(r, b, n), 0.0, [wk], ["X%d_%d" % (s, r)], n)

        for ch in range(NP):
            head(ch)
        for ch in range(NP):
            body(ch)
            if ch > 0:
                tail(ch - 1)
        tail(NP - 1)
        if not last:
            update()
            nsent += (len(cuts) - 1) * (2 * hf + len(e_near))
            low[0] = -C["low"]
            prep(t + 1)
        if t in (1, 2, 3, 4):
            decode(t % 4)
        low[0] = 0.0
    wait("g", [("lsD", nsent)], [], after=[(gq[0], 0.0)])
    _emit(g, T, ops)
